import numpy as np
import ml_dtypes


def mxq(x, axis, fmt="e4m3"):
    dtype, down = {"e4m3": (ml_dtypes.float8_e4m3fn, 7), "e5m2": (ml_dtypes.float8_e5m2, 14)}[fmt]
    v = np.moveaxis(np.asarray(x, np.float32).astype(ml_dtypes.bfloat16).astype(np.float64), axis, -1)
    blocks = v.reshape(v.shape[:-1] + (-1, 32))
    amax = np.abs(blocks).max(-1, keepdims=True)
    byte = np.maximum(np.where(amax > 0, np.frexp(amax)[1] - 1 + 127, 0) - down, 1)
    scale = np.exp2(byte - 127.0)
    codes = (blocks / scale).astype(np.float32).astype(dtype).astype(np.float64)
    return np.moveaxis((codes * scale).reshape(v.shape), -1, axis)


WIDE = False


def mx_kscale(k):
    if not WIDE:
        return np.ones(k)
    levels = np.array([10, -10, 5, -5, 0])
    if k % 512:
        return np.exp2(np.random.permutation(np.resize(levels, k // 32))).repeat(32)
    a = np.empty((k // 512, 16))
    for p in range(k // 512):
        a[p, :8] = np.random.permutation(np.resize(levels, 8))
        for g in range(8):
            far = levels[np.abs(levels - a[p, g]) >= 10]
            a[p, g + 8] = far[np.random.randint(len(far))]
    return np.exp2(a.ravel()).repeat(32)


def f64(x):
    return np.asarray(x).astype(np.float64)


def striped(idx):
    return np.tile(np.asarray(idx).reshape(-1, 16).T, (8, 1)).astype(np.uint16)


def unstriped(offs):
    return offs[:16].T.reshape(-1).astype(np.int64)


E2M1 = np.array([0.0, 0.5, 1.0, 1.5, 2.0, 3.0, 4.0, 6.0, -0.0, -0.5, -1.0, -1.5, -2.0, -3.0, -4.0, -6.0])


def pack_weight(w, fmt):
    k, n = w.shape
    w = f64(np.asarray(w, np.float32).astype(ml_dtypes.bfloat16)).reshape(k // 32, 32, n)
    amax = np.abs(w).max(1)
    if fmt == "e4m3":
        byte = np.frexp(amax)[1] - 1 + 127 - 7
    else:
        mant, ex = np.frexp(amax / 6.0)
        byte = np.where(mant > 0.5, ex, ex - 1) + 127
    byte = np.clip(np.where(amax > 0, byte, 1), 1, 254)
    scaled = (w * np.exp2(127.0 - byte)[:, None, :]).reshape(k, n).astype(np.float32)
    by_word = np.ascontiguousarray(scaled.reshape(k // 512, 128, 4, n).transpose(0, 1, 3, 2))
    if fmt == "e4m3":
        words = by_word.astype(ml_dtypes.float8_e4m3fn).view(np.uint8)
    else:
        c = by_word.astype(ml_dtypes.float4_e2m1fn).view(np.uint8) & 0xF
        words = (c[..., 0::2] | (c[..., 1::2] << 4)).reshape(k // 512, 128, 2 * n)
    return np.ascontiguousarray(words), np.ascontiguousarray(byte.astype(np.uint8).reshape(k // 512, 16, n))


def unpack_weight(words, scales, fmt):
    g, _, n = scales.shape
    words = np.ascontiguousarray(words).reshape(g, 128, n, -1)
    if fmt == "e4m3":
        vals = words.view(ml_dtypes.float8_e4m3fn).astype(np.float64)
    else:
        nib = np.empty((g, 128, n, 4), np.uint8)
        nib[..., 0::2] = words & 0xF
        nib[..., 1::2] = words >> 4
        vals = E2M1[nib]
    vals = vals * np.repeat(np.exp2(scales.astype(np.float64) - 127.0), 8, axis=1)[..., None]
    return vals.transpose(0, 1, 3, 2).reshape(g * 512, n)


B, N, T, D, DV, NQ = 1, 512, 1024, 512, 128, 256


def setup_inputs():
    n = np.random.standard_normal
    idx = np.random.permutation(T)[:B * N]
    s = mx_kscale(D)[:, None]
    u = np.ones(T)
    u[idx] = mx_kscale(B * N)
    r = np.random.uniform(0.5, 2.0, T)
    k = n((D, T)) / s
    v = n((DV, T)) / (u * r)
    kp = pack_weight(k, "e4m3")
    return {
        "qT": (n((B, D, NQ)) * s * (0.80 / np.sqrt(D))).astype(np.float32),
        "k_words": kp[0],
        "k_scales": kp[1],
        "vT": v.astype(np.float32),
        "vs": np.tile(u * r, (128, 1)).astype(np.float32),
        "kb": np.tile(n(T), (128, 1)).astype(np.float32),
        "og": n((B, NQ, DV)).astype(np.float32),
        "offs": striped(idx),
    }


def reference(qT, k_words, k_scales, vT, vs, kb, og, offs):
    idx = unstriped(offs)
    k = unpack_weight(k_words, k_scales, "e4m3")
    v = f64(vT)
    pick = lambda x: x[:, idx].reshape(x.shape[0], B, N).transpose(1, 0, 2)
    q = f64(qT)
    score = mxq(q, 1, "e4m3").transpose(0, 2, 1) @ pick(k)
    score = score + pick(f64(kb))[:, :1, :]
    m = score.max(-1, keepdims=True)
    p = np.exp(score - m)
    total = p.sum(-1, keepdims=True)
    w = p * pick(f64(vs))[:, :1, :]
    y = mxq(w, 2, "e4m3") @ mxq(pick(v).transpose(0, 2, 1), 1, "e4m3")
    y = y / total
    y = y / (1.0 + np.exp(-f64(og)))
    return y

@@ -1,0 +1,189 @@
+from contextlib import ExitStack
+
+import concourse.mybir as mybir
+from concourse.masks import make_identity
+
+F32 = mybir.dt.float32
+BF16 = mybir.dt.bfloat16
+I32 = mybir.dt.int32
+U32 = mybir.dt.uint32
+U16 = mybir.dt.uint16
+U8 = mybir.dt.uint8
+FP8X4 = mybir.dt.float8_e4m3fn_x4
+ACT = mybir.ActivationFunctionType
+ALU = mybir.AluOpType
+
+P = 128
+PACK = 4
+SLOTS = 512
+POOL = 1024
+NQ = 256
+DV = 128
+CHUNKS = SLOTS // P
+QBLOCKS = NQ // P
+LIST_COLS = P // 16
+
+FLOPS = 2 * NQ * SLOTS * 512 + 2 * NQ * SLOTS * DV
+
+
+def tile_attend_bias_gate_topk_kernel(tc, qT, k_words, k_scales, vT, vs, kb, og, offs, out):
+    nc = tc.nc
+    with ExitStack() as ctx:
+        sb = ctx.enter_context(tc.tile_pool(name="sb", bufs=1))
+        ps = ctx.enter_context(tc.psum_pool(name="ps", bufs=1))
+
+        offsets = sb.tile([P, SLOTS // 16], U16, name="offsets")
+        nc.sync.dma_start(offsets[:], offs)
+
+        def chunk_offsets(c):
+            return offsets[:, c * LIST_COLS : (c + 1) * LIST_COLS]
+
+        ks_pool = sb.tile([P, POOL], U8, name="ks_pool", align_bytes=64)
+        kb_pool = sb.tile([P, POOL], F32, name="kb_pool")
+        vs_pool = sb.tile([P, POOL], F32, name="vs_pool")
+        nc.vector.memset(ks_pool[:].bitcast(I32), 0)
+        nc.vector.memset(kb_pool[:], 0.0)
+        scale_rows = k_scales[0].rearrange("(q r) n -> r q n", r=4)
+        for r in range(4):
+            nc.scalar.dma_start(ks_pool[r:P:32, :].bitcast(I32), scale_rows[r].bitcast(I32))
+        nc.scalar.dma_start(kb_pool[0:1, :], kb[0:1, :])
+
+        q_raw = sb.tile([P, PACK, NQ], F32, name="q_raw", tag="staging")
+        nc.sync.dma_start(q_raw[:], qT[0].rearrange("(p t) q -> p t q", t=PACK))
+        kw_pool = sb.tile([P, POOL], I32, name="kw_pool", align_bytes=64)
+        nc.sync.dma_start(kw_pool[:], k_words[0].rearrange("p n t -> p (n t)").bitcast(I32))
+
+        ident = sb.tile([P, P], F32, name="ident")
+        make_identity(nc, ident[:])
+        nc.gpsimd.memset(vs_pool[:], 0.0)
+        nc.gpsimd.dma_start(vs_pool[0:1, :], vs[0:1, :])
+        og_sb = sb.tile([P, QBLOCKS, DV], F32, name="og_sb")
+        nc.gpsimd.dma_start(og_sb[:], og[0].rearrange("(b q) e -> q b e", q=P))
+
+        k_scale = sb.tile([P, SLOTS], U8, name="k_scale", align_bytes=64)
+        nc.vector.tensor_copy(k_scale[:], ks_pool[:].indirect(offsets[:]))
+        kb_row = sb.tile([P, SLOTS], F32, name="kb_row")
+        nc.vector.tensor_copy(kb_row[:], kb_pool[:].indirect(offsets[:]))
+
+        q_bf = sb.tile([P, NQ, PACK], BF16, name="q_bf", align_bytes=64)
+        nc.scalar.copy(q_bf[:], q_raw[:].rearrange("p t q -> p q t"))
+        v_pool = sb.tile([P, POOL], F32, name="v_pool", tag="staging")
+        nc.sync.dma_start(v_pool[:], vT)
+        q_codes = sb.tile([P, NQ], U32, name="q_codes", align_bytes=64)
+        q_scale = sb.tile([P, NQ], U8, name="q_scale", align_bytes=64)
+        nc.vector.quantize_mx(q_codes[:].bitcast(FP8X4), q_scale[:], q_bf[:].rearrange("p q t -> p (q t)"))
+
+        kb_turned = ps.tile([P, CHUNKS, P], F32, name="kb_turned", tag="col0")
+        for c in range(CHUNKS):
+            nc.tensor.transpose(kb_turned[:, c, :], kb_row[:, c * P : (c + 1) * P], ident[:])
+        neg_kb = sb.tile([P, CHUNKS], F32, name="neg_kb")
+        nc.scalar.activation(neg_kb[:], kb_turned[:, :, 0], ACT.Copy, scale=-1.0)
+
+        k_codes = sb.tile([P, SLOTS], U32, name="k_codes", align_bytes=64)
+        neg_rows = [ps.tile([P, SLOTS], F32, name="neg_rows%d" % b, tag="row%d" % b) for b in range(QBLOCKS)]
+        neg_cols = []
+        for c in range(CHUNKS):
+            cols = slice(c * P, (c + 1) * P)
+            nc.vector.tensor_copy(k_codes[:, cols], kw_pool[:].bitcast(U32).indirect(chunk_offsets(c)))
+            scores = ps.tile([P, NQ], F32, name="scores%d" % c, tag="sc%d" % c)
+            nc.tensor.matmul_mx(
+                scores[:],
+                lhsT=k_codes[:, cols].bitcast(FP8X4),
+                lhsT_scale=k_scale[:, cols],
+                rhs=q_codes[:].bitcast(FP8X4),
+                rhs_scale=q_scale[:],
+                start=True,
+                stop=True,
+            )
+            neg = sb.tile([P, NQ], F32, name="neg_cols%d" % c)
+            nc.scalar.activation(neg[:], scores[:], ACT.Identity, bias=neg_kb[:, c : c + 1], scale=-1.0)
+            neg_cols.append(neg)
+        for c in range(CHUNKS):
+            for b in range(QBLOCKS):
+                nc.tensor.transpose(neg_rows[b][:, c * P : (c + 1) * P], neg_cols[c][:, b * P : (b + 1) * P], ident[:])
+
+        vs_row = sb.tile([P, SLOTS], F32, name="vs_row")
+        nc.vector.tensor_copy(vs_row[:], vs_pool[:].indirect(offsets[:]))
+
+        neg_max = [sb.tile([P, 1], F32, name="neg_max%d" % b) for b in range(QBLOCKS)]
+        total = sb.tile([P, QBLOCKS], F32, name="total")
+        p_rows = []
+        for b in range(QBLOCKS):
+            nc.vector.tensor_reduce(neg_max[b][:], neg_rows[b][:], mybir.AxisListType.X, ALU.min)
+            p_row = sb.tile([P, PACK, P], F32, name="p_row%d" % b)
+            nc.scalar.activation(
+                p_row[:],
+                neg_rows[b][:].rearrange("q (s t) -> q t s", t=PACK),
+                ACT.Exp,
+                bias=neg_max[b][:],
+                scale=-1.0,
+                accum_out=total[:, b : b + 1],
+            )
+            p_rows.append(p_row)
+
+        vs_turned = ps.tile([P, PACK, P], F32, name="vs_turned", tag="sc3")
+        for t in range(PACK):
+            nc.tensor.transpose(vs_turned[:, t, :], vs_row[:, t:SLOTS:PACK], ident[:])
+        vs_col = sb.tile([P, PACK], F32, name="vs_col")
+        nc.scalar.copy(vs_col[:], vs_turned[:, :, 0])
+
+        p_cols = []
+        for b in range(QBLOCKS):
+            p_col = ps.tile([P, PACK, P], F32, name="p_col%d" % b, tag="col%d" % b)
+            for t in range(PACK):
+                nc.tensor.transpose(p_col[:, t, :], p_rows[b][:, t, :], ident[:])
+            p_cols.append(p_col)
+
+        w_bf = [sb.tile([P, P, PACK], BF16, name="w_bf%d" % b, align_bytes=64) for b in range(QBLOCKS)]
+        for b in range(QBLOCKS):
+            nc.vector.tensor_tensor(
+                w_bf[b][:],
+                p_cols[b][:].rearrange("s t q -> s q t"),
+                vs_col[:].unsqueeze(1).to_broadcast([P, P, PACK]),
+                ALU.mult,
+            )
+
+        v_pairs = sb.tile([P, 2, P, 2], BF16, name="v_pairs")
+        for c in range(CHUNKS):
+            s = slice(c * (P // PACK), (c + 1) * (P // PACK))
+            nc.vector.tensor_copy(
+                v_pairs[:, :, s, :].rearrange("e u s i -> e s u i"), v_pool[:].indirect(chunk_offsets(c))
+            )
+        v_words = v_pairs[:].rearrange("e u s i -> e u (s i)").bitcast(F32)
+        v_turned = ps.tile([P, 2, DV], F32, name="v_turned", tag="sc0")
+        for u in range(2):
+            nc.tensor.transpose(v_turned[:, u, :], v_words[:, u, :], ident[:])
+        v_bf = sb.tile([P, DV * PACK], BF16, name="v_bf", align_bytes=64)
+        nc.scalar.copy(
+            v_bf[:].bitcast(F32).rearrange("s (e u) -> s e u", u=2), v_turned[:].rearrange("s u e -> s e u")
+        )
+        v_codes = sb.tile([P, DV], U32, name="v_codes", align_bytes=64)
+        v_scale = sb.tile([P, DV], U8, name="v_scale", align_bytes=64)
+        nc.vector.quantize_mx(v_codes[:].bitcast(FP8X4), v_scale[:], v_bf[:])
+
+        half_tanh = sb.tile([P, QBLOCKS, DV], F32, name="half_tanh")
+        nc.scalar.activation(half_tanh[:], og_sb[:], ACT.Tanh, scale=0.5)
+        gate = sb.tile([P, QBLOCKS, DV], F32, name="gate")
+        nc.scalar.activation(gate[:], half_tanh[:], ACT.Copy, bias=0.5, scale=0.5)
+        inv_total = sb.tile([P, QBLOCKS], F32, name="inv_total")
+        nc.vector.reciprocal(inv_total[:], total[:])
+
+        for b in range(QBLOCKS):
+            w_codes = sb.tile([P, P], U32, name="w_codes%d" % b, align_bytes=64)
+            w_scale = sb.tile([P, P], U8, name="w_scale%d" % b, align_bytes=64)
+            nc.vector.quantize_mx(w_codes[:].bitcast(FP8X4), w_scale[:], w_bf[b][:].rearrange("s q t -> s (q t)"))
+            sums = ps.tile([P, DV], F32, name="sums%d" % b, tag="sc%d" % (b + 1))
+            nc.tensor.matmul_mx(
+                sums[:],
+                lhsT=w_codes[:].bitcast(FP8X4),
+                lhsT_scale=w_scale[:],
+                rhs=v_codes[:].bitcast(FP8X4),
+                rhs_scale=v_scale[:],
+                start=True,
+                stop=True,
+            )
+            result = sb.tile([P, DV], F32, name="result%d" % b)
+            nc.vector.scalar_tensor_tensor(
+                result[:], sums[:], inv_total[:, b : b + 1], gate[:, b, :], ALU.mult, ALU.mult
+            )
+            nc.sync.dma_start(out[0, b * P : (b + 1) * P, :], result[:])

@@ -22,6 +22,7 @@ DV = 128
 CHUNKS = SLOTS // P
 QBLOCKS = NQ // P
 LIST_COLS = P // 16
+WARM_UPS = 12
 
 FLOPS = 2 * NQ * SLOTS * 512 + 2 * NQ * SLOTS * DV
 
@@ -41,24 +42,32 @@ def tile_attend_bias_gate_topk_kernel(tc, qT, k_words, k_scales, vT, vs, kb, og,
         ks_pool = sb.tile([P, POOL], U8, name="ks_pool", align_bytes=64)
         kb_pool = sb.tile([P, POOL], F32, name="kb_pool")
         vs_pool = sb.tile([P, POOL], F32, name="vs_pool")
-        nc.vector.memset(ks_pool[:].bitcast(I32), 0)
-        nc.vector.memset(kb_pool[:], 0.0)
+        nc.gpsimd.memset(ks_pool[:].bitcast(I32), 0)
+        nc.gpsimd.memset(kb_pool[:, : POOL // 2], 0.0)
+        nc.vector.memset(kb_pool[:, POOL // 2 :], 0.0)
+        nc.vector.memset(vs_pool[:], 0.0)
         scale_rows = k_scales[0].rearrange("(q r) n -> r q n", r=4)
         for r in range(4):
-            nc.scalar.dma_start(ks_pool[r:P:32, :].bitcast(I32), scale_rows[r].bitcast(I32))
-        nc.scalar.dma_start(kb_pool[0:1, :], kb[0:1, :])
+            nc.sync.dma_start(ks_pool[r:P:32, :].bitcast(I32), scale_rows[r].bitcast(I32))
+        nc.sync.dma_start(kb_pool[0:1, :], kb[0:1, :])
 
-        q_raw = sb.tile([P, PACK, NQ], F32, name="q_raw", tag="staging")
+        q_raw = sb.tile([P, PACK, NQ], F32, name="q_raw")
         nc.sync.dma_start(q_raw[:], qT[0].rearrange("(p t) q -> p t q", t=PACK))
         kw_pool = sb.tile([P, POOL], I32, name="kw_pool", align_bytes=64)
         nc.sync.dma_start(kw_pool[:], k_words[0].rearrange("p n t -> p (n t)").bitcast(I32))
+        og_sb = sb.tile([P, QBLOCKS, DV], F32, name="og_sb")
+        nc.sync.dma_start(og_sb[:], og[0].rearrange("(b q) e -> q b e", q=P))
+        nc.sync.dma_start(vs_pool[0:1, :], vs[0:1, :])
+        v_pool = sb.tile([P, POOL], F32, name="v_pool")
+        nc.sync.dma_start(v_pool[:], vT)
 
         ident = sb.tile([P, P], F32, name="ident")
         make_identity(nc, ident[:])
-        nc.gpsimd.memset(vs_pool[:], 0.0)
-        nc.gpsimd.dma_start(vs_pool[0:1, :], vs[0:1, :])
-        og_sb = sb.tile([P, QBLOCKS, DV], F32, name="og_sb")
-        nc.gpsimd.dma_start(og_sb[:], og[0].rearrange("(b q) e -> q b e", q=P))
+
+        for b in range(QBLOCKS):
+            warm = ps.tile([P, CHUNKS, P], F32, name="warm%d" % b, tag="row%d" % b)
+            for i in range(WARM_UPS):
+                nc.tensor.transpose(warm[:, i % CHUNKS, :], ident[:], ident[:])
 
         k_scale = sb.tile([P, SLOTS], U8, name="k_scale", align_bytes=64)
         nc.vector.tensor_copy(k_scale[:], ks_pool[:].indirect(offsets[:]))
@@ -67,8 +76,6 @@ def tile_attend_bias_gate_topk_kernel(tc, qT, k_words, k_scales, vT, vs, kb, og,
 
         q_bf = sb.tile([P, NQ, PACK], BF16, name="q_bf", align_bytes=64)
         nc.scalar.copy(q_bf[:], q_raw[:].rearrange("p t q -> p q t"))
-        v_pool = sb.tile([P, POOL], F32, name="v_pool", tag="staging")
-        nc.sync.dma_start(v_pool[:], vT)
         q_codes = sb.tile([P, NQ], U32, name="q_codes", align_bytes=64)
         q_scale = sb.tile([P, NQ], U8, name="q_scale", align_bytes=64)
         nc.vector.quantize_mx(q_codes[:].bitcast(FP8X4), q_scale[:], q_bf[:].rearrange("p q t -> p (q t)"))
@@ -106,20 +113,26 @@ def tile_attend_bias_gate_topk_kernel(tc, qT, k_words, k_scales, vT, vs, kb, og,
         nc.vector.tensor_copy(vs_row[:], vs_pool[:].indirect(offsets[:]))
 
         neg_max = [sb.tile([P, 1], F32, name="neg_max%d" % b) for b in range(QBLOCKS)]
-        total = sb.tile([P, QBLOCKS], F32, name="total")
+        part_total = sb.tile([P, 2, QBLOCKS], F32, name="part_total")
         p_rows = []
         for b in range(QBLOCKS):
             nc.vector.tensor_reduce(neg_max[b][:], neg_rows[b][:], mybir.AxisListType.X, ALU.min)
             p_row = sb.tile([P, PACK, P], F32, name="p_row%d" % b)
-            nc.scalar.activation(
-                p_row[:],
-                neg_rows[b][:].rearrange("q (s t) -> q t s", t=PACK),
-                ACT.Exp,
-                bias=neg_max[b][:],
-                scale=-1.0,
-                accum_out=total[:, b : b + 1],
-            )
+            for u in range(2):
+                nc.scalar.activation(
+                    p_row[:, 2 * u : 2 * u + 2, :],
+                    neg_rows[b][:].rearrange("q (s t) -> q t s", t=PACK)[:, 2 * u : 2 * u + 2, :],
+                    ACT.Exp,
+                    bias=neg_max[b][:],
+                    scale=-1.0,
+                    accum_out=part_total[:, u, b : b + 1],
+                )
             p_rows.append(p_row)
+
+        inv_total = sb.tile([P, QBLOCKS], F32, name="inv_total")
+        total = sb.tile([P, QBLOCKS], F32, name="total")
+        nc.vector.tensor_tensor(total[:], part_total[:, 0, :], part_total[:, 1, :], ALU.add)
+        nc.vector.reciprocal(inv_total[:], total[:])
 
         vs_turned = ps.tile([P, PACK, P], F32, name="vs_turned", tag="sc3")
         for t in range(PACK):
@@ -164,9 +177,9 @@ def tile_attend_bias_gate_topk_kernel(tc, qT, k_words, k_scales, vT, vs, kb, og,
         half_tanh = sb.tile([P, QBLOCKS, DV], F32, name="half_tanh")
         nc.scalar.activation(half_tanh[:], og_sb[:], ACT.Tanh, scale=0.5)
         gate = sb.tile([P, QBLOCKS, DV], F32, name="gate")
-        nc.scalar.activation(gate[:], half_tanh[:], ACT.Copy, bias=0.5, scale=0.5)
-        inv_total = sb.tile([P, QBLOCKS], F32, name="inv_total")
-        nc.vector.reciprocal(inv_total[:], total[:])
+        for b in range(QBLOCKS):
+            inv = inv_total[:, b : b + 1]
+            nc.scalar.activation(gate[:, b, :], half_tanh[:, b, :], ACT.Identity, bias=inv, scale=inv)
 
         for b in range(QBLOCKS):
             w_codes = sb.tile([P, P], U32, name="w_codes%d" % b, align_bytes=64)
@@ -184,6 +197,6 @@ def tile_attend_bias_gate_topk_kernel(tc, qT, k_words, k_scales, vT, vs, kb, og,
             )
             result = sb.tile([P, DV], F32, name="result%d" % b)
             nc.vector.scalar_tensor_tensor(
-                result[:], sums[:], inv_total[:, b : b + 1], gate[:, b, :], ALU.mult, ALU.mult
+                result[:], sums[:], 0.5, gate[:, b, :], ALU.mult, ALU.mult
             )
             nc.sync.dma_start(out[0, b * P : (b + 1) * P, :], result[:])

@@ -1,4 +1,5 @@
 from contextlib import ExitStack
+from itertools import product
 
 import concourse.mybir as mybir
 from concourse.masks import make_identity
@@ -23,6 +24,8 @@ CHUNKS = SLOTS // P
 QBLOCKS = NQ // P
 LIST_COLS = P // 16
 WARM_UPS = 12
+LAG = 1
+KEY_PIECES = {0: 2, 2: 3, 3: 4}
 
 FLOPS = 2 * NQ * SLOTS * 512 + 2 * NQ * SLOTS * DV
 
@@ -36,9 +39,6 @@ def tile_attend_bias_gate_topk_kernel(tc, qT, k_words, k_scales, vT, vs, kb, og,
         offsets = sb.tile([P, SLOTS // 16], U16, name="offsets")
         nc.sync.dma_start(offsets[:], offs)
 
-        def chunk_offsets(c):
-            return offsets[:, c * LIST_COLS : (c + 1) * LIST_COLS]
-
         ks_pool = sb.tile([P, POOL], U8, name="ks_pool", align_bytes=64)
         kb_pool = sb.tile([P, POOL], F32, name="kb_pool")
         vs_pool = sb.tile([P, POOL], F32, name="vs_pool")
@@ -48,18 +48,19 @@ def tile_attend_bias_gate_topk_kernel(tc, qT, k_words, k_scales, vT, vs, kb, og,
         nc.vector.memset(vs_pool[:], 0.0)
         scale_rows = k_scales[0].rearrange("(q r) n -> r q n", r=4)
         for r in range(4):
-            nc.sync.dma_start(ks_pool[r:P:32, :].bitcast(I32), scale_rows[r].bitcast(I32))
+            queue = nc.sync if r < 2 else nc.scalar
+            queue.dma_start(ks_pool[r:P:32, :].bitcast(I32), scale_rows[r].bitcast(I32))
         nc.sync.dma_start(kb_pool[0:1, :], kb[0:1, :])
 
         q_raw = sb.tile([P, PACK, NQ], F32, name="q_raw")
         nc.sync.dma_start(q_raw[:], qT[0].rearrange("(p t) q -> p t q", t=PACK))
-        kw_pool = sb.tile([P, POOL], I32, name="kw_pool", align_bytes=64)
+        kw_pool = sb.tile([P, POOL], I32, name="kw_pool", tag="kw_pool", align_bytes=64)
         nc.sync.dma_start(kw_pool[:], k_words[0].rearrange("p n t -> p (n t)").bitcast(I32))
-        og_sb = sb.tile([P, QBLOCKS, DV], F32, name="og_sb")
-        nc.sync.dma_start(og_sb[:], og[0].rearrange("(b q) e -> q b e", q=P))
         nc.sync.dma_start(vs_pool[0:1, :], vs[0:1, :])
         v_pool = sb.tile([P, POOL], F32, name="v_pool")
         nc.sync.dma_start(v_pool[:], vT)
+        og_sb = sb.tile([P, QBLOCKS, DV], F32, name="og_sb")
+        nc.sync.dma_start(og_sb[:], og[0].rearrange("(b q) e -> q b e", q=P))
 
         ident = sb.tile([P, P], F32, name="ident")
         make_identity(nc, ident[:])
@@ -74,7 +75,7 @@ def tile_attend_bias_gate_topk_kernel(tc, qT, k_words, k_scales, vT, vs, kb, og,
         kb_row = sb.tile([P, SLOTS], F32, name="kb_row")
         nc.vector.tensor_copy(kb_row[:], kb_pool[:].indirect(offsets[:]))
 
-        q_bf = sb.tile([P, NQ, PACK], BF16, name="q_bf", align_bytes=64)
+        q_bf = sb.tile([P, NQ, PACK], BF16, name="q_bf", tag="q_bf", align_bytes=64)
         nc.scalar.copy(q_bf[:], q_raw[:].rearrange("p t q -> p q t"))
         q_codes = sb.tile([P, NQ], U32, name="q_codes", align_bytes=64)
         q_scale = sb.tile([P, NQ], U8, name="q_scale", align_bytes=64)
@@ -86,30 +87,40 @@ def tile_attend_bias_gate_topk_kernel(tc, qT, k_words, k_scales, vT, vs, kb, og,
         neg_kb = sb.tile([P, CHUNKS], F32, name="neg_kb")
         nc.scalar.activation(neg_kb[:], kb_turned[:, :, 0], ACT.Copy, scale=-1.0)
 
-        k_codes = sb.tile([P, SLOTS], U32, name="k_codes", align_bytes=64)
+        k_codes = [
+            sb.tile([P, 2 * P], U32, name="k_codes0", align_bytes=64),
+            sb.tile([P, 2 * P], U32, name="k_codes1", tag="q_bf", align_bytes=64),
+        ]
         neg_rows = [ps.tile([P, SLOTS], F32, name="neg_rows%d" % b, tag="row%d" % b) for b in range(QBLOCKS)]
-        neg_cols = []
+        neg_cols, all_scores = [], []
         for c in range(CHUNKS):
             cols = slice(c * P, (c + 1) * P)
-            nc.vector.tensor_copy(k_codes[:, cols], kw_pool[:].bitcast(U32).indirect(chunk_offsets(c)))
+            if c in KEY_PIECES:
+                end = KEY_PIECES[c]
+                nc.vector.tensor_copy(
+                    k_codes[c // 2][:, c % 2 * P : (c % 2 + end - c) * P],
+                    kw_pool[:].bitcast(U32).indirect(offsets[:, c * LIST_COLS : end * LIST_COLS]),
+                )
             scores = ps.tile([P, NQ], F32, name="scores%d" % c, tag="sc%d" % c)
             nc.tensor.matmul_mx(
                 scores[:],
-                lhsT=k_codes[:, cols].bitcast(FP8X4),
+                lhsT=k_codes[c // 2][:, c % 2 * P : (c % 2 + 1) * P].bitcast(FP8X4),
                 lhsT_scale=k_scale[:, cols],
                 rhs=q_codes[:].bitcast(FP8X4),
                 rhs_scale=q_scale[:],
                 start=True,
                 stop=True,
             )
-            neg = sb.tile([P, NQ], F32, name="neg_cols%d" % c)
-            nc.scalar.activation(neg[:], scores[:], ACT.Identity, bias=neg_kb[:, c : c + 1], scale=-1.0)
-            neg_cols.append(neg)
-        for c in range(CHUNKS):
-            for b in range(QBLOCKS):
-                nc.tensor.transpose(neg_rows[b][:, c * P : (c + 1) * P], neg_cols[c][:, b * P : (b + 1) * P], ident[:])
+            all_scores.append(scores)
+            neg_cols.append(sb.tile([P, NQ], F32, name="neg_cols%d" % c, tag="neg_cols%d" % c))
+        for c, b in sorted(product(range(CHUNKS), range(QBLOCKS)), key=lambda cb: (cb[0] + LAG * cb[1], cb[1])):
+            rows = slice(b * P, (b + 1) * P)
+            nc.scalar.activation(
+                neg_cols[c][:, rows], all_scores[c][:, rows], ACT.Identity, bias=neg_kb[:, c : c + 1], scale=-1.0
+            )
+            nc.tensor.transpose(neg_rows[b][:, c * P : (c + 1) * P], neg_cols[c][:, rows], ident[:])
 
-        vs_row = sb.tile([P, SLOTS], F32, name="vs_row")
+        vs_row = sb.tile([P, SLOTS], F32, name="vs_row", tag="kw_pool", align_bytes=64)
         nc.vector.tensor_copy(vs_row[:], vs_pool[:].indirect(offsets[:]))
 
         neg_max = [sb.tile([P, 1], F32, name="neg_max%d" % b) for b in range(QBLOCKS)]
@@ -117,7 +128,7 @@ def tile_attend_bias_gate_topk_kernel(tc, qT, k_words, k_scales, vT, vs, kb, og,
         p_rows = []
         for b in range(QBLOCKS):
             nc.vector.tensor_reduce(neg_max[b][:], neg_rows[b][:], mybir.AxisListType.X, ALU.min)
-            p_row = sb.tile([P, PACK, P], F32, name="p_row%d" % b)
+            p_row = sb.tile([P, PACK, P], F32, name="p_row%d" % b, tag="p_row%d" % b)
             for u in range(2):
                 nc.scalar.activation(
                     p_row[:, 2 * u : 2 * u + 2, :],
@@ -129,16 +140,11 @@ def tile_attend_bias_gate_topk_kernel(tc, qT, k_words, k_scales, vT, vs, kb, og,
                 )
             p_rows.append(p_row)
 
-        inv_total = sb.tile([P, QBLOCKS], F32, name="inv_total")
-        total = sb.tile([P, QBLOCKS], F32, name="total")
-        nc.vector.tensor_tensor(total[:], part_total[:, 0, :], part_total[:, 1, :], ALU.add)
-        nc.vector.reciprocal(inv_total[:], total[:])
-
         vs_turned = ps.tile([P, PACK, P], F32, name="vs_turned", tag="sc3")
         for t in range(PACK):
             nc.tensor.transpose(vs_turned[:, t, :], vs_row[:, t:SLOTS:PACK], ident[:])
         vs_col = sb.tile([P, PACK], F32, name="vs_col")
-        nc.scalar.copy(vs_col[:], vs_turned[:, :, 0])
+        nc.vector.tensor_copy(vs_col[:], vs_turned[:, :, 0])
 
         p_cols = []
         for b in range(QBLOCKS):
@@ -156,14 +162,10 @@ def tile_attend_bias_gate_topk_kernel(tc, qT, k_words, k_scales, vT, vs, kb, og,
                 ALU.mult,
             )
 
-        v_pairs = sb.tile([P, 2, P, 2], BF16, name="v_pairs")
-        for c in range(CHUNKS):
-            s = slice(c * (P // PACK), (c + 1) * (P // PACK))
-            nc.vector.tensor_copy(
-                v_pairs[:, :, s, :].rearrange("e u s i -> e s u i"), v_pool[:].indirect(chunk_offsets(c))
-            )
+        v_pairs = sb.tile([P, 2, P, 2], BF16, name="v_pairs", tag="neg_cols3")
+        nc.vector.tensor_copy(v_pairs[:].rearrange("e u s i -> e s u i"), v_pool[:].indirect(offsets[:]))
         v_words = v_pairs[:].rearrange("e u s i -> e u (s i)").bitcast(F32)
-        v_turned = ps.tile([P, 2, DV], F32, name="v_turned", tag="sc0")
+        v_turned = ps.tile([P, 2, DV], F32, name="v_turned", tag="row1")
         for u in range(2):
             nc.tensor.transpose(v_turned[:, u, :], v_words[:, u, :], ident[:])
         v_bf = sb.tile([P, DV * PACK], BF16, name="v_bf", align_bytes=64)
@@ -174,20 +176,18 @@ def tile_attend_bias_gate_topk_kernel(tc, qT, k_words, k_scales, vT, vs, kb, og,
         v_scale = sb.tile([P, DV], U8, name="v_scale", align_bytes=64)
         nc.vector.quantize_mx(v_codes[:].bitcast(FP8X4), v_scale[:], v_bf[:])
 
-        half_tanh = sb.tile([P, QBLOCKS, DV], F32, name="half_tanh")
+        half_tanh = sb.tile([P, QBLOCKS, DV], F32, name="half_tanh", tag="p_row0")
         nc.scalar.activation(half_tanh[:], og_sb[:], ACT.Tanh, scale=0.5)
         gate = sb.tile([P, QBLOCKS, DV], F32, name="gate")
-        for b in range(QBLOCKS):
-            inv = inv_total[:, b : b + 1]
-            nc.scalar.activation(gate[:, b, :], half_tanh[:, b, :], ACT.Identity, bias=inv, scale=inv)
+        nc.scalar.activation(gate[:], half_tanh[:], ACT.Copy, bias=0.5, scale=0.5)
 
+        sums = [ps.tile([P, DV], F32, name="sums%d" % b, tag="sc%d" % (b + 1)) for b in range(QBLOCKS)]
         for b in range(QBLOCKS):
             w_codes = sb.tile([P, P], U32, name="w_codes%d" % b, align_bytes=64)
             w_scale = sb.tile([P, P], U8, name="w_scale%d" % b, align_bytes=64)
             nc.vector.quantize_mx(w_codes[:].bitcast(FP8X4), w_scale[:], w_bf[b][:].rearrange("s q t -> s (q t)"))
-            sums = ps.tile([P, DV], F32, name="sums%d" % b, tag="sc%d" % (b + 1))
             nc.tensor.matmul_mx(
-                sums[:],
+                sums[b][:],
                 lhsT=w_codes[:].bitcast(FP8X4),
                 lhsT_scale=w_scale[:],
                 rhs=v_codes[:].bitcast(FP8X4),
@@ -195,8 +195,14 @@ def tile_attend_bias_gate_topk_kernel(tc, qT, k_words, k_scales, vT, vs, kb, og,
                 start=True,
                 stop=True,
             )
+
+        inv_total = sb.tile([P, QBLOCKS], F32, name="inv_total")
+        total = sb.tile([P, QBLOCKS], F32, name="total")
+        nc.vector.tensor_tensor(total[:], part_total[:, 0, :], part_total[:, 1, :], ALU.add)
+        nc.vector.reciprocal(inv_total[:], total[:])
+        for b in range(QBLOCKS):
             result = sb.tile([P, DV], F32, name="result%d" % b)
             nc.vector.scalar_tensor_tensor(
-                result[:], sums[:], 0.5, gate[:, b, :], ALU.mult, ALU.mult
+                result[:], sums[b][:], inv_total[:, b : b + 1], gate[:, b, :], ALU.mult, ALU.mult
             )
             nc.sync.dma_start(out[0, b * P : (b + 1) * P, :], result[:])

@@ -1,5 +1,4 @@
 from contextlib import ExitStack
-from itertools import product
 
 import concourse.mybir as mybir
 from concourse.masks import make_identity
@@ -23,9 +22,7 @@ DV = 128
 CHUNKS = SLOTS // P
 QBLOCKS = NQ // P
 LIST_COLS = P // 16
-WARM_UPS = 12
-LAG = 1
-KEY_PIECES = {0: 2, 2: 3, 3: 4}
+ROW = P - 1
 
 FLOPS = 2 * NQ * SLOTS * 512 + 2 * NQ * SLOTS * DV
 
@@ -34,48 +31,44 @@ def tile_attend_bias_gate_topk_kernel(tc, qT, k_words, k_scales, vT, vs, kb, og,
     nc = tc.nc
     with ExitStack() as ctx:
         sb = ctx.enter_context(tc.tile_pool(name="sb", bufs=1))
+        shared = ctx.enter_context(tc.tile_pool(name="shared", bufs=1))
         ps = ctx.enter_context(tc.psum_pool(name="ps", bufs=1))
 
         offsets = sb.tile([P, SLOTS // 16], U16, name="offsets")
         nc.sync.dma_start(offsets[:], offs)
 
-        ks_pool = sb.tile([P, POOL], U8, name="ks_pool", align_bytes=64)
-        kb_pool = sb.tile([P, POOL], F32, name="kb_pool")
+        ks_pool = sb.tile([P, POOL], U8, name="ks_pool", tag="ks_pool", align_bytes=64)
+        kb_pool = sb.tile([P, POOL], F32, name="kb_pool", tag="kb_pool")
         vs_pool = sb.tile([P, POOL], F32, name="vs_pool")
         nc.gpsimd.memset(ks_pool[:].bitcast(I32), 0)
-        nc.gpsimd.memset(kb_pool[:, : POOL // 2], 0.0)
-        nc.vector.memset(kb_pool[:, POOL // 2 :], 0.0)
-        nc.vector.memset(vs_pool[:], 0.0)
+        nc.vector.memset(kb_pool[0:ROW, :], 0.0)
+        nc.gpsimd.memset(vs_pool[:, : POOL // 2], 0.0)
+        nc.vector.memset(vs_pool[:, POOL // 2 :], 0.0)
+        ident = sb.tile([P, P], F32, name="ident")
+        make_identity(nc, ident[:])
+        nc.sync.dma_start(kb_pool[ROW:P, :], kb[0:1, :])
+        q_raw = sb.tile([P, PACK, NQ], F32, name="q_raw", tag="q_raw", align_bytes=64)
+        nc.sync.dma_start(q_raw[:], qT[0].rearrange("(p t) q -> p t q", t=PACK))
         scale_rows = k_scales[0].rearrange("(q r) n -> r q n", r=4)
         for r in range(4):
             queue = nc.sync if r < 2 else nc.scalar
             queue.dma_start(ks_pool[r:P:32, :].bitcast(I32), scale_rows[r].bitcast(I32))
-        nc.sync.dma_start(kb_pool[0:1, :], kb[0:1, :])
 
-        q_raw = sb.tile([P, PACK, NQ], F32, name="q_raw")
-        nc.sync.dma_start(q_raw[:], qT[0].rearrange("(p t) q -> p t q", t=PACK))
         kw_pool = sb.tile([P, POOL], I32, name="kw_pool", tag="kw_pool", align_bytes=64)
         nc.sync.dma_start(kw_pool[:], k_words[0].rearrange("p n t -> p (n t)").bitcast(I32))
-        nc.sync.dma_start(vs_pool[0:1, :], vs[0:1, :])
-        v_pool = sb.tile([P, POOL], F32, name="v_pool")
-        nc.sync.dma_start(v_pool[:], vT)
-        og_sb = sb.tile([P, QBLOCKS, DV], F32, name="og_sb")
-        nc.sync.dma_start(og_sb[:], og[0].rearrange("(b q) e -> q b e", q=P))
+        nc.sync.dma_start(vs_pool[ROW:P, :], vs[0:1, :])
 
-        ident = sb.tile([P, P], F32, name="ident")
-        make_identity(nc, ident[:])
-
-        for b in range(QBLOCKS):
-            warm = ps.tile([P, CHUNKS, P], F32, name="warm%d" % b, tag="row%d" % b)
-            for i in range(WARM_UPS):
-                nc.tensor.transpose(warm[:, i % CHUNKS, :], ident[:], ident[:])
-
+        kb_row = shared.tile([P, SLOTS], F32, name="kb_row", offset=1024, align_bytes=64)
+        nc.vector.tensor_copy(kb_row[:], kb_pool[:].indirect(offsets[:]))
         k_scale = sb.tile([P, SLOTS], U8, name="k_scale", align_bytes=64)
         nc.vector.tensor_copy(k_scale[:], ks_pool[:].indirect(offsets[:]))
-        kb_row = sb.tile([P, SLOTS], F32, name="kb_row")
-        nc.vector.tensor_copy(kb_row[:], kb_pool[:].indirect(offsets[:]))
 
-        q_bf = sb.tile([P, NQ, PACK], BF16, name="q_bf", tag="q_bf", align_bytes=64)
+        v_pool = sb.tile([P, POOL], F32, name="v_pool", tag="kb_pool")
+        nc.sync.dma_start(v_pool[:], vT)
+        og_sb = sb.tile([P, QBLOCKS, DV], F32, name="og_sb", tag="ks_pool", align_bytes=64)
+        nc.sync.dma_start(og_sb[:], og[0].rearrange("(b q) e -> q b e", q=P))
+
+        q_bf = sb.tile([P, NQ, PACK], BF16, name="q_bf", align_bytes=64)
         nc.scalar.copy(q_bf[:], q_raw[:].rearrange("p t q -> p q t"))
         q_codes = sb.tile([P, NQ], U32, name="q_codes", align_bytes=64)
         q_scale = sb.tile([P, NQ], U8, name="q_scale", align_bytes=64)
@@ -84,67 +77,64 @@ def tile_attend_bias_gate_topk_kernel(tc, qT, k_words, k_scales, vT, vs, kb, og,
         kb_turned = ps.tile([P, CHUNKS, P], F32, name="kb_turned", tag="col0")
         for c in range(CHUNKS):
             nc.tensor.transpose(kb_turned[:, c, :], kb_row[:, c * P : (c + 1) * P], ident[:])
-        neg_kb = sb.tile([P, CHUNKS], F32, name="neg_kb")
-        nc.scalar.activation(neg_kb[:], kb_turned[:, :, 0], ACT.Copy, scale=-1.0)
+        kb_col = sb.tile([P, CHUNKS], F32, name="kb_col")
+        nc.scalar.copy(kb_col[:], kb_turned[:, :, ROW])
 
-        k_codes = [
-            sb.tile([P, 2 * P], U32, name="k_codes0", align_bytes=64),
-            sb.tile([P, 2 * P], U32, name="k_codes1", tag="q_bf", align_bytes=64),
-        ]
-        neg_rows = [ps.tile([P, SLOTS], F32, name="neg_rows%d" % b, tag="row%d" % b) for b in range(QBLOCKS)]
-        neg_cols, all_scores = [], []
+        k_picked = shared.tile([P, SLOTS], U32, name="k_picked", offset=0, align_bytes=64)
+        raw_cols = {}
         for c in range(CHUNKS):
             cols = slice(c * P, (c + 1) * P)
-            if c in KEY_PIECES:
-                end = KEY_PIECES[c]
-                nc.vector.tensor_copy(
-                    k_codes[c // 2][:, c % 2 * P : (c % 2 + end - c) * P],
-                    kw_pool[:].bitcast(U32).indirect(offsets[:, c * LIST_COLS : end * LIST_COLS]),
+            k_codes = k_picked[:, cols]
+            nc.vector.tensor_copy(
+                k_codes, kw_pool[:].bitcast(U32).indirect(offsets[:, c * LIST_COLS : (c + 1) * LIST_COLS])
+            )
+            width = NQ if c < CHUNKS - 1 else P
+            for q0 in range(0, NQ, width):
+                label = "%d_%d" % (c, q0)
+                scores = ps.tile([P, width], F32, name="scores" + label, tag="sc" + label)
+                nc.tensor.matmul_mx(
+                    scores[:],
+                    lhsT=k_codes.bitcast(FP8X4),
+                    lhsT_scale=k_scale[:, cols],
+                    rhs=q_codes[:, q0 : q0 + width].bitcast(FP8X4),
+                    rhs_scale=q_scale[:, q0 : q0 + width],
+                    start=True,
+                    stop=True,
                 )
-            scores = ps.tile([P, NQ], F32, name="scores%d" % c, tag="sc%d" % c)
-            nc.tensor.matmul_mx(
-                scores[:],
-                lhsT=k_codes[c // 2][:, c % 2 * P : (c % 2 + 1) * P].bitcast(FP8X4),
-                lhsT_scale=k_scale[:, cols],
-                rhs=q_codes[:].bitcast(FP8X4),
-                rhs_scale=q_scale[:],
-                start=True,
-                stop=True,
-            )
-            all_scores.append(scores)
-            neg_cols.append(sb.tile([P, NQ], F32, name="neg_cols%d" % c, tag="neg_cols%d" % c))
-        for c, b in sorted(product(range(CHUNKS), range(QBLOCKS)), key=lambda cb: (cb[0] + LAG * cb[1], cb[1])):
-            rows = slice(b * P, (b + 1) * P)
-            nc.scalar.activation(
-                neg_cols[c][:, rows], all_scores[c][:, rows], ACT.Identity, bias=neg_kb[:, c : c + 1], scale=-1.0
-            )
-            nc.tensor.transpose(neg_rows[b][:, c * P : (c + 1) * P], neg_cols[c][:, rows], ident[:])
+                for b in range(q0 // P, (q0 + width) // P):
+                    raw_cols[c, b] = scores[:, b * P - q0 : (b + 1) * P - q0]
 
-        vs_row = sb.tile([P, SLOTS], F32, name="vs_row", tag="kw_pool", align_bytes=64)
+        s_rows = []
+        for b, tag in enumerate(("row0", "sc3_0")):
+            s_row = ps.tile([P, SLOTS], F32, name="s_row%d" % b, tag=tag)
+            for c in range(CHUNKS):
+                label = "biased%d_%d" % (c, b)
+                biased = sb.tile([P, P], F32, name=label, tag=label, align_bytes=64)
+                nc.scalar.activation(biased[:], raw_cols[c, b], ACT.Identity, bias=kb_col[:, c : c + 1])
+                nc.tensor.transpose(s_row[:, c * P : (c + 1) * P], biased[:], ident[:])
+            s_rows.append(s_row)
+
+        vs_row = shared.tile([P, SLOTS], F32, name="vs_row", offset=2048, align_bytes=64)
         nc.vector.tensor_copy(vs_row[:], vs_pool[:].indirect(offsets[:]))
 
-        neg_max = [sb.tile([P, 1], F32, name="neg_max%d" % b) for b in range(QBLOCKS)]
-        part_total = sb.tile([P, 2, QBLOCKS], F32, name="part_total")
+        neg_max = [sb.tile([P, 1], F32, name="neg_max%d" % b, tag="neg_max%d" % b) for b in range(QBLOCKS)]
+        total = sb.tile([P, QBLOCKS], F32, name="total")
         p_rows = []
         for b in range(QBLOCKS):
-            nc.vector.tensor_reduce(neg_max[b][:], neg_rows[b][:], mybir.AxisListType.X, ALU.min)
-            p_row = sb.tile([P, PACK, P], F32, name="p_row%d" % b, tag="p_row%d" % b)
-            for u in range(2):
-                nc.scalar.activation(
-                    p_row[:, 2 * u : 2 * u + 2, :],
-                    neg_rows[b][:].rearrange("q (s t) -> q t s", t=PACK)[:, 2 * u : 2 * u + 2, :],
-                    ACT.Exp,
-                    bias=neg_max[b][:],
-                    scale=-1.0,
-                    accum_out=part_total[:, u, b : b + 1],
-                )
+            nc.vector.tensor_reduce(neg_max[b][:], s_rows[b][:], mybir.AxisListType.X, ALU.max, negate=True)
+            p_row = sb.tile([P, PACK, P], F32, name="p_row%d" % b, tag="p_row%d" % b, align_bytes=64)
+            nc.scalar.activation(
+                p_row[:],
+                s_rows[b][:].rearrange("q (s t) -> q t s", t=PACK),
+                ACT.Exp,
+                bias=neg_max[b][:],
+                accum_out=total[:, b : b + 1],
+            )
             p_rows.append(p_row)
 
-        vs_turned = ps.tile([P, PACK, P], F32, name="vs_turned", tag="sc3")
+        vs_turned = ps.tile([P, PACK, P], F32, name="vs_turned", tag="sc3_128")
         for t in range(PACK):
             nc.tensor.transpose(vs_turned[:, t, :], vs_row[:, t:SLOTS:PACK], ident[:])
-        vs_col = sb.tile([P, PACK], F32, name="vs_col")
-        nc.vector.tensor_copy(vs_col[:], vs_turned[:, :, 0])
 
         p_cols = []
         for b in range(QBLOCKS):
@@ -152,6 +142,20 @@ def tile_attend_bias_gate_topk_kernel(tc, qT, k_words, k_scales, vT, vs, kb, og,
             for t in range(PACK):
                 nc.tensor.transpose(p_col[:, t, :], p_rows[b][:, t, :], ident[:])
             p_cols.append(p_col)
+
+        v_picked = sb.tile([P, SLOTS], BF16, name="v_picked", tag="biased3_1", align_bytes=64)
+        nc.vector.tensor_copy(v_picked[:], v_pool[:].indirect(offsets[:]))
+        v_words = v_picked[:].bitcast(F32)
+        v_turned = ps.tile([P, 2, DV], F32, name="v_turned", tag="sc3_0")
+        for u in range(2):
+            nc.tensor.transpose(v_turned[:, u, :], v_words[:, u : SLOTS // 2 : 2], ident[:])
+        v_bf = sb.tile([P, DV * PACK], BF16, name="v_bf", align_bytes=64)
+        nc.scalar.copy(
+            v_bf[:].bitcast(F32).rearrange("s (e u) -> s e u", u=2), v_turned[:].rearrange("s u e -> s e u")
+        )
+
+        vs_col = sb.tile([P, PACK], F32, name="vs_col", tag="neg_max0")
+        nc.scalar.copy(vs_col[:], vs_turned[:, :, ROW])
 
         w_bf = [sb.tile([P, P, PACK], BF16, name="w_bf%d" % b, align_bytes=64) for b in range(QBLOCKS)]
         for b in range(QBLOCKS):
@@ -162,30 +166,23 @@ def tile_attend_bias_gate_topk_kernel(tc, qT, k_words, k_scales, vT, vs, kb, og,
                 ALU.mult,
             )
 
-        v_pairs = sb.tile([P, 2, P, 2], BF16, name="v_pairs", tag="neg_cols3")
-        nc.vector.tensor_copy(v_pairs[:].rearrange("e u s i -> e s u i"), v_pool[:].indirect(offsets[:]))
-        v_words = v_pairs[:].rearrange("e u s i -> e u (s i)").bitcast(F32)
-        v_turned = ps.tile([P, 2, DV], F32, name="v_turned", tag="row1")
-        for u in range(2):
-            nc.tensor.transpose(v_turned[:, u, :], v_words[:, u, :], ident[:])
-        v_bf = sb.tile([P, DV * PACK], BF16, name="v_bf", align_bytes=64)
-        nc.scalar.copy(
-            v_bf[:].bitcast(F32).rearrange("s (e u) -> s e u", u=2), v_turned[:].rearrange("s u e -> s e u")
-        )
-        v_codes = sb.tile([P, DV], U32, name="v_codes", align_bytes=64)
-        v_scale = sb.tile([P, DV], U8, name="v_scale", align_bytes=64)
-        nc.vector.quantize_mx(v_codes[:].bitcast(FP8X4), v_scale[:], v_bf[:])
-
-        half_tanh = sb.tile([P, QBLOCKS, DV], F32, name="half_tanh", tag="p_row0")
+        half_tanh = sb.tile([P, QBLOCKS, DV], F32, name="half_tanh", tag="p_row0", align_bytes=64)
         nc.scalar.activation(half_tanh[:], og_sb[:], ACT.Tanh, scale=0.5)
         gate = sb.tile([P, QBLOCKS, DV], F32, name="gate")
         nc.scalar.activation(gate[:], half_tanh[:], ACT.Copy, bias=0.5, scale=0.5)
 
-        sums = [ps.tile([P, DV], F32, name="sums%d" % b, tag="sc%d" % (b + 1)) for b in range(QBLOCKS)]
+        inv_total = sb.tile([P, QBLOCKS], F32, name="inv_total")
+        nc.vector.reciprocal(inv_total[:], total[:])
+
+        v_codes = sb.tile([P, DV], U32, name="v_codes", align_bytes=64)
+        v_scale = sb.tile([P, DV], U8, name="v_scale", align_bytes=64)
+        sums = [ps.tile([P, DV], F32, name="sums%d" % b, tag="sc%d_0" % b) for b in range(QBLOCKS)]
         for b in range(QBLOCKS):
-            w_codes = sb.tile([P, P], U32, name="w_codes%d" % b, align_bytes=64)
+            w_codes = sb.tile([P, P], U32, name="w_codes%d" % b, tag="p_row1" if b == 0 else "w_codes1", align_bytes=64)
             w_scale = sb.tile([P, P], U8, name="w_scale%d" % b, align_bytes=64)
             nc.vector.quantize_mx(w_codes[:].bitcast(FP8X4), w_scale[:], w_bf[b][:].rearrange("s q t -> s (q t)"))
+            if b == 0:
+                nc.vector.quantize_mx(v_codes[:].bitcast(FP8X4), v_scale[:], v_bf[:])
             nc.tensor.matmul_mx(
                 sums[b][:],
                 lhsT=w_codes[:].bitcast(FP8X4),
@@ -196,10 +193,6 @@ def tile_attend_bias_gate_topk_kernel(tc, qT, k_words, k_scales, vT, vs, kb, og,
                 stop=True,
             )
 
-        inv_total = sb.tile([P, QBLOCKS], F32, name="inv_total")
-        total = sb.tile([P, QBLOCKS], F32, name="total")
-        nc.vector.tensor_tensor(total[:], part_total[:, 0, :], part_total[:, 1, :], ALU.add)
-        nc.vector.reciprocal(inv_total[:], total[:])
         for b in range(QBLOCKS):
             result = sb.tile([P, DV], F32, name="result%d" % b)
             nc.vector.scalar_tensor_tensor(

@@ -23,6 +23,7 @@ CHUNKS = SLOTS // P
 QBLOCKS = NQ // P
 LIST_COLS = P // 16
 ROW = P - 1
+WIDE_CHUNKS = 2
 
 FLOPS = 2 * NQ * SLOTS * 512 + 2 * NQ * SLOTS * DV
 
@@ -54,6 +55,8 @@ def tile_attend_bias_gate_topk_kernel(tc, qT, k_words, k_scales, vT, vs, kb, og,
             queue = nc.sync if r < 2 else nc.scalar
             queue.dma_start(ks_pool[r:P:32, :].bitcast(I32), scale_rows[r].bitcast(I32))
 
+        v_raw = sb.tile([P, POOL], F32, name="v_raw")
+        nc.sync.dma_start(v_raw[:], vT)
         kw_pool = sb.tile([P, POOL], I32, name="kw_pool", tag="kw_pool", align_bytes=64)
         nc.sync.dma_start(kw_pool[:], k_words[0].rearrange("p n t -> p (n t)").bitcast(I32))
         nc.sync.dma_start(vs_pool[ROW:P, :], vs[0:1, :])
@@ -63,8 +66,6 @@ def tile_attend_bias_gate_topk_kernel(tc, qT, k_words, k_scales, vT, vs, kb, og,
         k_scale = sb.tile([P, SLOTS], U8, name="k_scale", align_bytes=64)
         nc.vector.tensor_copy(k_scale[:], ks_pool[:].indirect(offsets[:]))
 
-        v_pool = sb.tile([P, POOL], F32, name="v_pool", tag="kb_pool")
-        nc.sync.dma_start(v_pool[:], vT)
         og_sb = sb.tile([P, QBLOCKS, DV], F32, name="og_sb", tag="ks_pool", align_bytes=64)
         nc.sync.dma_start(og_sb[:], og[0].rearrange("(b q) e -> q b e", q=P))
 
@@ -74,6 +75,12 @@ def tile_attend_bias_gate_topk_kernel(tc, qT, k_words, k_scales, vT, vs, kb, og,
         q_scale = sb.tile([P, NQ], U8, name="q_scale", align_bytes=64)
         nc.vector.quantize_mx(q_codes[:].bitcast(FP8X4), q_scale[:], q_bf[:].rearrange("p q t -> p (q t)"))
 
+        v_pool = sb.tile([P, POOL], BF16, name="v_pool", align_bytes=64)
+        nc.scalar.activation(v_pool[:, : POOL // 2], v_raw[:, : POOL // 2], ACT.Copy)
+        nc.vector.tensor_copy(v_pool[:, POOL // 2 :], v_raw[:, POOL // 2 :])
+        v_picked = sb.tile([P, SLOTS], BF16, name="v_picked", align_bytes=64)
+        nc.scalar.activation(v_picked[:], v_pool[:].indirect(offsets[:]), ACT.Copy)
+
         kb_turned = ps.tile([P, CHUNKS, P], F32, name="kb_turned", tag="col0")
         for c in range(CHUNKS):
             nc.tensor.transpose(kb_turned[:, c, :], kb_row[:, c * P : (c + 1) * P], ident[:])
@@ -81,7 +88,7 @@ def tile_attend_bias_gate_topk_kernel(tc, qT, k_words, k_scales, vT, vs, kb, og,
         nc.scalar.copy(kb_col[:], kb_turned[:, :, ROW])
 
         k_picked = shared.tile([P, SLOTS], U32, name="k_picked", offset=0, align_bytes=64)
-        raw_cols = {}
+        raw_cols, s_cols = {}, {}
         for c in range(CHUNKS):
             cols = slice(c * P, (c + 1) * P)
             k_codes = k_picked[:, cols]
@@ -101,40 +108,58 @@ def tile_attend_bias_gate_topk_kernel(tc, qT, k_words, k_scales, vT, vs, kb, og,
                     start=True,
                     stop=True,
                 )
-                for b in range(q0 // P, (q0 + width) // P):
-                    raw_cols[c, b] = scores[:, b * P - q0 : (b + 1) * P - q0]
+                if c < WIDE_CHUNKS:
+                    wide = sb.tile([P, NQ], F32, name="wide%d" % c, align_bytes=64)
+                    nc.scalar.activation(wide[:], scores[:], ACT.Identity, bias=kb_col[:, c : c + 1])
+                    for b in range(QBLOCKS):
+                        s_cols[c, b] = wide[:, b * P : (b + 1) * P]
+                else:
+                    for b in range(q0 // P, (q0 + width) // P):
+                        raw_cols[c, b] = scores[:, b * P - q0 : (b + 1) * P - q0]
 
         s_rows = []
         for b, tag in enumerate(("row0", "sc3_0")):
             s_row = ps.tile([P, SLOTS], F32, name="s_row%d" % b, tag=tag)
             for c in range(CHUNKS):
-                label = "biased%d_%d" % (c, b)
-                biased = sb.tile([P, P], F32, name=label, tag=label, align_bytes=64)
-                nc.scalar.activation(biased[:], raw_cols[c, b], ACT.Identity, bias=kb_col[:, c : c + 1])
-                nc.tensor.transpose(s_row[:, c * P : (c + 1) * P], biased[:], ident[:])
+                if c >= WIDE_CHUNKS:
+                    biased = sb.tile([P, P], F32, name="biased%d_%d" % (c, b), align_bytes=64)
+                    nc.scalar.activation(biased[:], raw_cols[c, b], ACT.Identity, bias=kb_col[:, c : c + 1])
+                    s_cols[c, b] = biased[:]
+                nc.tensor.transpose(s_row[:, c * P : (c + 1) * P], s_cols[c, b], ident[:])
             s_rows.append(s_row)
 
         vs_row = shared.tile([P, SLOTS], F32, name="vs_row", offset=2048, align_bytes=64)
         nc.vector.tensor_copy(vs_row[:], vs_pool[:].indirect(offsets[:]))
+        vs_col = sb.tile([P, PACK], F32, name="vs_col", tag="vs_col")
+        nc.sync.dma_start(vs_col[:], vs_row[ROW:P, :].rearrange("o (s t) -> o s t", t=PACK))
 
         neg_max = [sb.tile([P, 1], F32, name="neg_max%d" % b, tag="neg_max%d" % b) for b in range(QBLOCKS)]
-        total = sb.tile([P, QBLOCKS], F32, name="total")
+        part_total = sb.tile([P, 2, QBLOCKS], F32, name="part_total")
         p_rows = []
         for b in range(QBLOCKS):
             nc.vector.tensor_reduce(neg_max[b][:], s_rows[b][:], mybir.AxisListType.X, ALU.max, negate=True)
             p_row = sb.tile([P, PACK, P], F32, name="p_row%d" % b, tag="p_row%d" % b, align_bytes=64)
-            nc.scalar.activation(
-                p_row[:],
-                s_rows[b][:].rearrange("q (s t) -> q t s", t=PACK),
-                ACT.Exp,
-                bias=neg_max[b][:],
-                accum_out=total[:, b : b + 1],
-            )
+            for u in range(2):
+                nc.scalar.activation(
+                    p_row[:, 2 * u : 2 * u + 2, :],
+                    s_rows[b][:].rearrange("q (s t) -> q t s", t=PACK)[:, 2 * u : 2 * u + 2, :],
+                    ACT.Exp,
+                    bias=neg_max[b][:],
+                    accum_out=part_total[:, u, b : b + 1],
+                )
             p_rows.append(p_row)
 
-        vs_turned = ps.tile([P, PACK, P], F32, name="vs_turned", tag="sc3_128")
-        for t in range(PACK):
-            nc.tensor.transpose(vs_turned[:, t, :], vs_row[:, t:SLOTS:PACK], ident[:])
+        v_words = v_picked[:].bitcast(F32)
+        v_turned = ps.tile([P, 2, DV], F32, name="v_turned", tag="sc3_128")
+        for u in range(2):
+            nc.tensor.transpose(v_turned[:, u, :], v_words[:, u : SLOTS // 2 : 2], ident[:])
+        v_bf = sb.tile([P, DV * PACK], BF16, name="v_bf", align_bytes=64)
+        nc.vector.tensor_copy(
+            v_bf[:].bitcast(F32).rearrange("s (e u) -> s e u", u=2), v_turned[:].rearrange("s u e -> s e u")
+        )
+        v_codes = sb.tile([P, DV], U32, name="v_codes", align_bytes=64)
+        v_scale = sb.tile([P, DV], U8, name="v_scale", align_bytes=64)
+        nc.vector.quantize_mx(v_codes[:].bitcast(FP8X4), v_scale[:], v_bf[:])
 
         p_cols = []
         for b in range(QBLOCKS):
@@ -142,20 +167,6 @@ def tile_attend_bias_gate_topk_kernel(tc, qT, k_words, k_scales, vT, vs, kb, og,
             for t in range(PACK):
                 nc.tensor.transpose(p_col[:, t, :], p_rows[b][:, t, :], ident[:])
             p_cols.append(p_col)
-
-        v_picked = sb.tile([P, SLOTS], BF16, name="v_picked", tag="biased3_1", align_bytes=64)
-        nc.vector.tensor_copy(v_picked[:], v_pool[:].indirect(offsets[:]))
-        v_words = v_picked[:].bitcast(F32)
-        v_turned = ps.tile([P, 2, DV], F32, name="v_turned", tag="sc3_0")
-        for u in range(2):
-            nc.tensor.transpose(v_turned[:, u, :], v_words[:, u : SLOTS // 2 : 2], ident[:])
-        v_bf = sb.tile([P, DV * PACK], BF16, name="v_bf", align_bytes=64)
-        nc.scalar.copy(
-            v_bf[:].bitcast(F32).rearrange("s (e u) -> s e u", u=2), v_turned[:].rearrange("s u e -> s e u")
-        )
-
-        vs_col = sb.tile([P, PACK], F32, name="vs_col", tag="neg_max0")
-        nc.scalar.copy(vs_col[:], vs_turned[:, :, ROW])
 
         w_bf = [sb.tile([P, P, PACK], BF16, name="w_bf%d" % b, align_bytes=64) for b in range(QBLOCKS)]
         for b in range(QBLOCKS):
@@ -171,18 +182,16 @@ def tile_attend_bias_gate_topk_kernel(tc, qT, k_words, k_scales, vT, vs, kb, og,
         gate = sb.tile([P, QBLOCKS, DV], F32, name="gate")
         nc.scalar.activation(gate[:], half_tanh[:], ACT.Copy, bias=0.5, scale=0.5)
 
-        inv_total = sb.tile([P, QBLOCKS], F32, name="inv_total")
+        total = sb.tile([P, QBLOCKS], F32, name="total")
+        nc.gpsimd.tensor_tensor(total[:], part_total[:, 0, :], part_total[:, 1, :], ALU.add)
+        inv_total = sb.tile([P, QBLOCKS], F32, name="inv_total", tag="vs_col")
         nc.vector.reciprocal(inv_total[:], total[:])
 
-        v_codes = sb.tile([P, DV], U32, name="v_codes", align_bytes=64)
-        v_scale = sb.tile([P, DV], U8, name="v_scale", align_bytes=64)
         sums = [ps.tile([P, DV], F32, name="sums%d" % b, tag="sc%d_0" % b) for b in range(QBLOCKS)]
         for b in range(QBLOCKS):
             w_codes = sb.tile([P, P], U32, name="w_codes%d" % b, tag="p_row1" if b == 0 else "w_codes1", align_bytes=64)
             w_scale = sb.tile([P, P], U8, name="w_scale%d" % b, align_bytes=64)
             nc.vector.quantize_mx(w_codes[:].bitcast(FP8X4), w_scale[:], w_bf[b][:].rearrange("s q t -> s (q t)"))
-            if b == 0:
-                nc.vector.quantize_mx(v_codes[:].bitcast(FP8X4), v_scale[:], v_bf[:])
             nc.tensor.matmul_mx(
                 sums[b][:],
                 lhsT=w_codes[:].bitcast(FP8X4),

@@ -1,7 +1,6 @@
 from contextlib import ExitStack
 
 import concourse.mybir as mybir
-from concourse.masks import make_identity
 
 F32 = mybir.dt.float32
 BF16 = mybir.dt.bfloat16
@@ -24,6 +23,7 @@ QBLOCKS = NQ // P
 LIST_COLS = P // 16
 ROW = P - 1
 WIDE_CHUNKS = 2
+QUAD = 32
 
 FLOPS = 2 * NQ * SLOTS * 512 + 2 * NQ * SLOTS * DV
 
@@ -43,12 +43,20 @@ def tile_attend_bias_gate_topk_kernel(tc, qT, k_words, k_scales, vT, vs, kb, og,
         vs_pool = sb.tile([P, POOL], F32, name="vs_pool")
         nc.gpsimd.memset(ks_pool[:].bitcast(I32), 0)
         nc.vector.memset(kb_pool[0:ROW, :], 0.0)
-        nc.gpsimd.memset(vs_pool[:, : POOL // 2], 0.0)
-        nc.vector.memset(vs_pool[:, POOL // 2 :], 0.0)
+        ones = sb.tile([P, P], F32, name="ones")
+        nc.gpsimd.memset(ones[:], 1.0)
+        quad_base = sb.tile([P, 1], F32, name="quad_base")
+        for first in range(0, P, QUAD):
+            nc.gpsimd.memset(quad_base[first : first + QUAD, :], float(first))
+        nc.gpsimd.memset(vs_pool[:], 0.0)
+        ramp = sb.tile([P, P], F32, name="ramp", align_bytes=64)
+        nc.vector.tensor_tensor_scan(ramp[:], ones[:], ones[:], 0.0, ALU.add, ALU.mult)
+        ramp_turned = sb.tile([P, QUAD], F32, name="ramp_turned", align_bytes=64)
+        nc.vector.transpose(ramp_turned[:], ramp[:, :QUAD])
         ident = sb.tile([P, P], F32, name="ident")
-        make_identity(nc, ident[:])
+        nc.vector.tensor_scalar(ident[:], ramp[:], quad_base[:], ramp_turned[:, 0:1], ALU.subtract, ALU.is_equal)
         nc.sync.dma_start(kb_pool[ROW:P, :], kb[0:1, :])
-        q_raw = sb.tile([P, PACK, NQ], F32, name="q_raw", tag="q_raw", align_bytes=64)
+        q_raw = shared.tile([P, PACK, NQ], F32, name="q_raw", offset=4096, align_bytes=64)
         nc.sync.dma_start(q_raw[:], qT[0].rearrange("(p t) q -> p t q", t=PACK))
         scale_rows = k_scales[0].rearrange("(q r) n -> r q n", r=4)
         for r in range(4):
@@ -84,7 +92,7 @@ def tile_attend_bias_gate_topk_kernel(tc, qT, k_words, k_scales, vT, vs, kb, og,
         kb_turned = ps.tile([P, CHUNKS, P], F32, name="kb_turned", tag="col0")
         for c in range(CHUNKS):
             nc.tensor.transpose(kb_turned[:, c, :], kb_row[:, c * P : (c + 1) * P], ident[:])
-        kb_col = sb.tile([P, CHUNKS], F32, name="kb_col")
+        kb_col = shared.tile([P, CHUNKS], F32, name="kb_col", offset=4096, align_bytes=64)
         nc.scalar.copy(kb_col[:], kb_turned[:, :, ROW])
 
         k_picked = shared.tile([P, SLOTS], U32, name="k_picked", offset=0, align_bytes=64)
@@ -183,7 +191,10 @@ def tile_attend_bias_gate_topk_kernel(tc, qT, k_words, k_scales, vT, vs, kb, og,
         nc.scalar.activation(gate[:], half_tanh[:], ACT.Copy, bias=0.5, scale=0.5)
 
         total = sb.tile([P, QBLOCKS], F32, name="total")
-        nc.gpsimd.tensor_tensor(total[:], part_total[:, 0, :], part_total[:, 1, :], ALU.add)
+        for b in range(QBLOCKS):
+            nc.scalar.activation(
+                total[:, b : b + 1], part_total[:, 0, b : b + 1], ACT.Identity, bias=part_total[:, 1, b : b + 1]
+            )
         inv_total = sb.tile([P, QBLOCKS], F32, name="inv_total", tag="vs_col")
         nc.vector.reciprocal(inv_total[:], total[:])
 

@@ -1,6 +1,7 @@
 from contextlib import ExitStack
 
 import concourse.mybir as mybir
+from concourse.masks import make_identity
 
 F32 = mybir.dt.float32
 BF16 = mybir.dt.bfloat16
@@ -23,7 +24,7 @@ QBLOCKS = NQ // P
 LIST_COLS = P // 16
 ROW = P - 1
 WIDE_CHUNKS = 2
-QUAD = 32
+EARLY = 320
 
 FLOPS = 2 * NQ * SLOTS * 512 + 2 * NQ * SLOTS * DV
 
@@ -41,20 +42,11 @@ def tile_attend_bias_gate_topk_kernel(tc, qT, k_words, k_scales, vT, vs, kb, og,
         ks_pool = sb.tile([P, POOL], U8, name="ks_pool", tag="ks_pool", align_bytes=64)
         kb_pool = sb.tile([P, POOL], F32, name="kb_pool", tag="kb_pool")
         vs_pool = sb.tile([P, POOL], F32, name="vs_pool")
-        nc.gpsimd.memset(ks_pool[:].bitcast(I32), 0)
+        nc.vector.memset(ks_pool[:].bitcast(I32), 0)
         nc.vector.memset(kb_pool[0:ROW, :], 0.0)
-        ones = sb.tile([P, P], F32, name="ones")
-        nc.gpsimd.memset(ones[:], 1.0)
-        quad_base = sb.tile([P, 1], F32, name="quad_base")
-        for first in range(0, P, QUAD):
-            nc.gpsimd.memset(quad_base[first : first + QUAD, :], float(first))
-        nc.gpsimd.memset(vs_pool[:], 0.0)
-        ramp = sb.tile([P, P], F32, name="ramp", align_bytes=64)
-        nc.vector.tensor_tensor_scan(ramp[:], ones[:], ones[:], 0.0, ALU.add, ALU.mult)
-        ramp_turned = sb.tile([P, QUAD], F32, name="ramp_turned", align_bytes=64)
-        nc.vector.transpose(ramp_turned[:], ramp[:, :QUAD])
+        nc.vector.memset(vs_pool[:], 0.0)
         ident = sb.tile([P, P], F32, name="ident")
-        nc.vector.tensor_scalar(ident[:], ramp[:], quad_base[:], ramp_turned[:, 0:1], ALU.subtract, ALU.is_equal)
+        make_identity(nc, ident[:])
         nc.sync.dma_start(kb_pool[ROW:P, :], kb[0:1, :])
         q_raw = shared.tile([P, PACK, NQ], F32, name="q_raw", offset=4096, align_bytes=64)
         nc.sync.dma_start(q_raw[:], qT[0].rearrange("(p t) q -> p t q", t=PACK))
@@ -84,10 +76,9 @@ def tile_attend_bias_gate_topk_kernel(tc, qT, k_words, k_scales, vT, vs, kb, og,
         nc.vector.quantize_mx(q_codes[:].bitcast(FP8X4), q_scale[:], q_bf[:].rearrange("p q t -> p (q t)"))
 
         v_pool = sb.tile([P, POOL], BF16, name="v_pool", align_bytes=64)
-        nc.scalar.activation(v_pool[:, : POOL // 2], v_raw[:, : POOL // 2], ACT.Copy)
-        nc.vector.tensor_copy(v_pool[:, POOL // 2 :], v_raw[:, POOL // 2 :])
-        v_picked = sb.tile([P, SLOTS], BF16, name="v_picked", align_bytes=64)
-        nc.scalar.activation(v_picked[:], v_pool[:].indirect(offsets[:]), ACT.Copy)
+        nc.scalar.activation(v_pool[:], v_raw[:], ACT.Copy)
+        v_picked = sb.tile([P, EARLY + 2 * P], BF16, name="v_picked", align_bytes=64)
+        nc.scalar.activation(v_picked[:, :EARLY], v_pool[:].indirect(offsets[:, : EARLY // 16]), ACT.Copy)
 
         kb_turned = ps.tile([P, CHUNKS, P], F32, name="kb_turned", tag="col0")
         for c in range(CHUNKS):
@@ -130,11 +121,15 @@ def tile_attend_bias_gate_topk_kernel(tc, qT, k_words, k_scales, vT, vs, kb, og,
             s_row = ps.tile([P, SLOTS], F32, name="s_row%d" % b, tag=tag)
             for c in range(CHUNKS):
                 if c >= WIDE_CHUNKS:
-                    biased = sb.tile([P, P], F32, name="biased%d_%d" % (c, b), align_bytes=64)
-                    nc.scalar.activation(biased[:], raw_cols[c, b], ACT.Identity, bias=kb_col[:, c : c + 1])
-                    s_cols[c, b] = biased[:]
+                    if (c, b) == (WIDE_CHUNKS, 0):
+                        s_cols[c, b] = v_picked[:, EARLY:].bitcast(F32)
+                    else:
+                        s_cols[c, b] = sb.tile([P, P], F32, name="biased%d_%d" % (c, b), align_bytes=64)[:]
+                    nc.scalar.activation(s_cols[c, b], raw_cols[c, b], ACT.Identity, bias=kb_col[:, c : c + 1])
                 nc.tensor.transpose(s_row[:, c * P : (c + 1) * P], s_cols[c, b], ident[:])
             s_rows.append(s_row)
+
+        nc.scalar.activation(v_picked[:, EARLY:SLOTS], v_pool[:].indirect(offsets[:, EARLY // 16 :]), ACT.Copy)
 
         vs_row = shared.tile([P, SLOTS], F32, name="vs_row", offset=2048, align_bytes=64)
         nc.vector.tensor_copy(vs_row[:], vs_pool[:].indirect(offsets[:]))

@@ -47,7 +47,7 @@ def tile_attend_bias_gate_topk_kernel(tc, qT, k_words, k_scales, vT, vs, kb, og,
         nc.vector.memset(vs_pool[:], 0.0)
         ident = sb.tile([P, P], F32, name="ident")
         make_identity(nc, ident[:])
-        nc.sync.dma_start(kb_pool[ROW:P, :], kb[0:1, :])
+        nc.scalar.dma_start(kb_pool[ROW:P, :], kb[0:1, :])
         q_raw = shared.tile([P, PACK, NQ], F32, name="q_raw", offset=4096, align_bytes=64)
         nc.sync.dma_start(q_raw[:], qT[0].rearrange("(p t) q -> p t q", t=PACK))
         scale_rows = k_scales[0].rearrange("(q r) n -> r q n", r=4)
@@ -70,7 +70,9 @@ def tile_attend_bias_gate_topk_kernel(tc, qT, k_words, k_scales, vT, vs, kb, og,
         nc.sync.dma_start(og_sb[:], og[0].rearrange("(b q) e -> q b e", q=P))
 
         q_bf = sb.tile([P, NQ, PACK], BF16, name="q_bf", align_bytes=64)
-        nc.scalar.copy(q_bf[:], q_raw[:].rearrange("p t q -> p q t"))
+        nc.scalar.copy(
+            q_bf[:].rearrange("p (c i) t -> p c t i", i=4), q_raw[:].rearrange("p t (c i) -> p c t i", i=4)
+        )
         q_codes = sb.tile([P, NQ], U32, name="q_codes", align_bytes=64)
         q_scale = sb.tile([P, NQ], U8, name="q_scale", align_bytes=64)
         nc.vector.quantize_mx(q_codes[:].bitcast(FP8X4), q_scale[:], q_bf[:].rearrange("p q t -> p (q t)"))
@@ -161,8 +163,7 @@ def tile_attend_bias_gate_topk_kernel(tc, qT, k_words, k_scales, vT, vs, kb, og,
             v_bf[:].bitcast(F32).rearrange("s (e u) -> s e u", u=2), v_turned[:].rearrange("s u e -> s e u")
         )
         v_codes = sb.tile([P, DV], U32, name="v_codes", align_bytes=64)
-        v_scale = sb.tile([P, DV], U8, name="v_scale", align_bytes=64)
-        nc.vector.quantize_mx(v_codes[:].bitcast(FP8X4), v_scale[:], v_bf[:])
+        v_scale = shared.tile([P, DV], U8, name="v_scale", offset=3072, align_bytes=64)
 
         p_cols = []
         for b in range(QBLOCKS):
@@ -179,6 +180,8 @@ def tile_attend_bias_gate_topk_kernel(tc, qT, k_words, k_scales, vT, vs, kb, og,
                 vs_col[:].unsqueeze(1).to_broadcast([P, P, PACK]),
                 ALU.mult,
             )
+            if b == 0:
+                nc.vector.quantize_mx(v_codes[:].bitcast(FP8X4), v_scale[:], v_bf[:])
 
         half_tanh = sb.tile([P, QBLOCKS, DV], F32, name="half_tanh", tag="p_row0", align_bytes=64)
         nc.scalar.activation(half_tanh[:], og_sb[:], ACT.Tanh, scale=0.5)
@@ -190,8 +193,6 @@ def tile_attend_bias_gate_topk_kernel(tc, qT, k_words, k_scales, vT, vs, kb, og,
             nc.scalar.activation(
                 total[:, b : b + 1], part_total[:, 0, b : b + 1], ACT.Identity, bias=part_total[:, 1, b : b + 1]
             )
-        inv_total = sb.tile([P, QBLOCKS], F32, name="inv_total", tag="vs_col")
-        nc.vector.reciprocal(inv_total[:], total[:])
 
         sums = [ps.tile([P, DV], F32, name="sums%d" % b, tag="sc%d_0" % b) for b in range(QBLOCKS)]
         for b in range(QBLOCKS):
@@ -207,6 +208,9 @@ def tile_attend_bias_gate_topk_kernel(tc, qT, k_words, k_scales, vT, vs, kb, og,
                 start=True,
                 stop=True,
             )
+
+        inv_total = sb.tile([P, QBLOCKS], F32, name="inv_total", tag="vs_col")
+        nc.vector.reciprocal(inv_total[:], total[:])
 
         for b in range(QBLOCKS):
             result = sb.tile([P, DV], F32, name="result%d" % b)

@@ -15,18 +15,29 @@ ALU = mybir.AluOpType
 
 P = 128
 PACK = 4
+QUADRANT = 32
+GROUP = 16
+LINE = 4
+D = 512
 SLOTS = 512
 POOL = 1024
 NQ = 256
 DV = 128
 CHUNKS = SLOTS // P
 QBLOCKS = NQ // P
-LIST_COLS = P // 16
 ROW = P - 1
+
 WIDE_CHUNKS = 2
 EARLY = 320
 
-FLOPS = 2 * NQ * SLOTS * 512 + 2 * NQ * SLOTS * DV
+ROW_BYTES = 4 * SLOTS
+KEYS_AT = 0
+BIAS_ROW_AT = ROW_BYTES // 2
+VS_ROW_AT = ROW_BYTES
+V_SCALE_AT = BIAS_ROW_AT + ROW_BYTES
+QUERIES_AT = 2 * ROW_BYTES
+
+FLOPS = 2 * NQ * SLOTS * D + 2 * NQ * SLOTS * DV
 
 
 def tile_attend_bias_gate_topk_kernel(tc, qT, k_words, k_scales, vT, vs, kb, og, offs, out):
@@ -36,32 +47,34 @@ def tile_attend_bias_gate_topk_kernel(tc, qT, k_words, k_scales, vT, vs, kb, og,
         shared = ctx.enter_context(tc.tile_pool(name="shared", bufs=1))
         ps = ctx.enter_context(tc.psum_pool(name="ps", bufs=1))
 
-        offsets = sb.tile([P, SLOTS // 16], U16, name="offsets")
+        offsets = sb.tile([P, SLOTS // GROUP], U16, name="offsets")
         nc.sync.dma_start(offsets[:], offs)
 
         ks_pool = sb.tile([P, POOL], U8, name="ks_pool", tag="ks_pool", align_bytes=64)
-        kb_pool = sb.tile([P, POOL], F32, name="kb_pool", tag="kb_pool")
+        kb_pool = sb.tile([P, POOL], F32, name="kb_pool")
         vs_pool = sb.tile([P, POOL], F32, name="vs_pool")
         nc.vector.memset(ks_pool[:].bitcast(I32), 0)
         nc.vector.memset(kb_pool[0:ROW, :], 0.0)
         nc.vector.memset(vs_pool[:], 0.0)
         ident = sb.tile([P, P], F32, name="ident")
-        make_identity(nc, ident[:])
+        nc.vector.memset(ident[:], 0.0)
+        make_identity(nc, ident[:], nomemset=True)
+
         nc.scalar.dma_start(kb_pool[ROW:P, :], kb[0:1, :])
-        q_raw = shared.tile([P, PACK, NQ], F32, name="q_raw", offset=4096, align_bytes=64)
+        q_raw = shared.tile([P, PACK, NQ], F32, name="q_raw", offset=QUERIES_AT, align_bytes=64)
         nc.sync.dma_start(q_raw[:], qT[0].rearrange("(p t) q -> p t q", t=PACK))
-        scale_rows = k_scales[0].rearrange("(q r) n -> r q n", r=4)
-        for r in range(4):
-            queue = nc.sync if r < 2 else nc.scalar
-            queue.dma_start(ks_pool[r:P:32, :].bitcast(I32), scale_rows[r].bitcast(I32))
+        scale_rows = k_scales[0].rearrange("(a r) n -> r a n", r=PACK)
+        for r in range(PACK):
+            queue = nc.sync if r < PACK // 2 else nc.scalar
+            queue.dma_start(ks_pool[r:P:QUADRANT, :].bitcast(I32), scale_rows[r].bitcast(I32))
 
         v_raw = sb.tile([P, POOL], F32, name="v_raw")
         nc.sync.dma_start(v_raw[:], vT)
-        kw_pool = sb.tile([P, POOL], I32, name="kw_pool", tag="kw_pool", align_bytes=64)
+        kw_pool = sb.tile([P, POOL], I32, name="kw_pool", align_bytes=64)
         nc.sync.dma_start(kw_pool[:], k_words[0].rearrange("p n t -> p (n t)").bitcast(I32))
         nc.sync.dma_start(vs_pool[ROW:P, :], vs[0:1, :])
 
-        kb_row = shared.tile([P, SLOTS], F32, name="kb_row", offset=1024, align_bytes=64)
+        kb_row = shared.tile([P, SLOTS], F32, name="kb_row", offset=BIAS_ROW_AT, align_bytes=64)
         nc.vector.tensor_copy(kb_row[:], kb_pool[:].indirect(offsets[:]))
         k_scale = sb.tile([P, SLOTS], U8, name="k_scale", align_bytes=64)
         nc.vector.tensor_copy(k_scale[:], ks_pool[:].indirect(offsets[:]))
@@ -71,7 +84,7 @@ def tile_attend_bias_gate_topk_kernel(tc, qT, k_words, k_scales, vT, vs, kb, og,
 
         q_bf = sb.tile([P, NQ, PACK], BF16, name="q_bf", align_bytes=64)
         nc.scalar.copy(
-            q_bf[:].rearrange("p (c i) t -> p c t i", i=4), q_raw[:].rearrange("p t (c i) -> p c t i", i=4)
+            q_bf[:].rearrange("p (c i) t -> p c t i", i=LINE), q_raw[:].rearrange("p t (c i) -> p c t i", i=LINE)
         )
         q_codes = sb.tile([P, NQ], U32, name="q_codes", align_bytes=64)
         q_scale = sb.tile([P, NQ], U8, name="q_scale", align_bytes=64)
@@ -80,21 +93,21 @@ def tile_attend_bias_gate_topk_kernel(tc, qT, k_words, k_scales, vT, vs, kb, og,
         v_pool = sb.tile([P, POOL], BF16, name="v_pool", align_bytes=64)
         nc.scalar.activation(v_pool[:], v_raw[:], ACT.Copy)
         v_picked = sb.tile([P, EARLY + 2 * P], BF16, name="v_picked", align_bytes=64)
-        nc.scalar.activation(v_picked[:, :EARLY], v_pool[:].indirect(offsets[:, : EARLY // 16]), ACT.Copy)
+        nc.scalar.activation(v_picked[:, :EARLY], v_pool[:].indirect(offsets[:, : EARLY // GROUP]), ACT.Copy)
 
         kb_turned = ps.tile([P, CHUNKS, P], F32, name="kb_turned", tag="col0")
         for c in range(CHUNKS):
             nc.tensor.transpose(kb_turned[:, c, :], kb_row[:, c * P : (c + 1) * P], ident[:])
-        kb_col = shared.tile([P, CHUNKS], F32, name="kb_col", offset=4096, align_bytes=64)
+        kb_col = shared.tile([P, CHUNKS], F32, name="kb_col", offset=QUERIES_AT, align_bytes=64)
         nc.scalar.copy(kb_col[:], kb_turned[:, :, ROW])
 
-        k_picked = shared.tile([P, SLOTS], U32, name="k_picked", offset=0, align_bytes=64)
-        raw_cols, s_cols = {}, {}
+        k_picked = shared.tile([P, SLOTS], U32, name="k_picked", offset=KEYS_AT, align_bytes=64)
+        in_psum, biased = {}, {}
         for c in range(CHUNKS):
             cols = slice(c * P, (c + 1) * P)
             k_codes = k_picked[:, cols]
             nc.vector.tensor_copy(
-                k_codes, kw_pool[:].bitcast(U32).indirect(offsets[:, c * LIST_COLS : (c + 1) * LIST_COLS])
+                k_codes, kw_pool[:].bitcast(U32).indirect(offsets[:, c * P // GROUP : (c + 1) * P // GROUP])
             )
             width = NQ if c < CHUNKS - 1 else P
             for q0 in range(0, NQ, width):
@@ -113,32 +126,34 @@ def tile_attend_bias_gate_topk_kernel(tc, qT, k_words, k_scales, vT, vs, kb, og,
                     wide = sb.tile([P, NQ], F32, name="wide%d" % c, align_bytes=64)
                     nc.scalar.activation(wide[:], scores[:], ACT.Identity, bias=kb_col[:, c : c + 1])
                     for b in range(QBLOCKS):
-                        s_cols[c, b] = wide[:, b * P : (b + 1) * P]
+                        biased[c, b] = wide[:, b * P : (b + 1) * P]
                 else:
                     for b in range(q0 // P, (q0 + width) // P):
-                        raw_cols[c, b] = scores[:, b * P - q0 : (b + 1) * P - q0]
+                        in_psum[c, b] = scores[:, b * P - q0 : (b + 1) * P - q0]
 
+        first_block_last_bank = "sc%d_%d" % (CHUNKS - 1, 0)
+        second_block_last_bank = "sc%d_%d" % (CHUNKS - 1, P)
         s_rows = []
-        for b, tag in enumerate(("row0", "sc3_0")):
+        for b, tag in enumerate(("row0", first_block_last_bank)):
             s_row = ps.tile([P, SLOTS], F32, name="s_row%d" % b, tag=tag)
             for c in range(CHUNKS):
                 if c >= WIDE_CHUNKS:
                     if (c, b) == (WIDE_CHUNKS, 0):
-                        s_cols[c, b] = v_picked[:, EARLY:].bitcast(F32)
+                        biased[c, b] = v_picked[:, EARLY:].bitcast(F32)
                     else:
-                        s_cols[c, b] = sb.tile([P, P], F32, name="biased%d_%d" % (c, b), align_bytes=64)[:]
-                    nc.scalar.activation(s_cols[c, b], raw_cols[c, b], ACT.Identity, bias=kb_col[:, c : c + 1])
-                nc.tensor.transpose(s_row[:, c * P : (c + 1) * P], s_cols[c, b], ident[:])
+                        biased[c, b] = sb.tile([P, P], F32, name="biased%d_%d" % (c, b), align_bytes=64)[:]
+                    nc.scalar.activation(biased[c, b], in_psum[c, b], ACT.Identity, bias=kb_col[:, c : c + 1])
+                nc.tensor.transpose(s_row[:, c * P : (c + 1) * P], biased[c, b], ident[:])
             s_rows.append(s_row)
 
-        nc.scalar.activation(v_picked[:, EARLY:SLOTS], v_pool[:].indirect(offsets[:, EARLY // 16 :]), ACT.Copy)
+        nc.scalar.activation(v_picked[:, EARLY:SLOTS], v_pool[:].indirect(offsets[:, EARLY // GROUP :]), ACT.Copy)
 
-        vs_row = shared.tile([P, SLOTS], F32, name="vs_row", offset=2048, align_bytes=64)
+        vs_row = shared.tile([P, SLOTS], F32, name="vs_row", offset=VS_ROW_AT, align_bytes=64)
         nc.vector.tensor_copy(vs_row[:], vs_pool[:].indirect(offsets[:]))
         vs_col = sb.tile([P, PACK], F32, name="vs_col", tag="vs_col")
         nc.sync.dma_start(vs_col[:], vs_row[ROW:P, :].rearrange("o (s t) -> o s t", t=PACK))
 
-        neg_max = [sb.tile([P, 1], F32, name="neg_max%d" % b, tag="neg_max%d" % b) for b in range(QBLOCKS)]
+        neg_max = [sb.tile([P, 1], F32, name="neg_max%d" % b) for b in range(QBLOCKS)]
         part_total = sb.tile([P, 2, QBLOCKS], F32, name="part_total")
         p_rows = []
         for b in range(QBLOCKS):
@@ -155,7 +170,7 @@ def tile_attend_bias_gate_topk_kernel(tc, qT, k_words, k_scales, vT, vs, kb, og,
             p_rows.append(p_row)
 
         v_words = v_picked[:].bitcast(F32)
-        v_turned = ps.tile([P, 2, DV], F32, name="v_turned", tag="sc3_128")
+        v_turned = ps.tile([P, 2, DV], F32, name="v_turned", tag=second_block_last_bank)
         for u in range(2):
             nc.tensor.transpose(v_turned[:, u, :], v_words[:, u : SLOTS // 2 : 2], ident[:])
         v_bf = sb.tile([P, DV * PACK], BF16, name="v_bf", align_bytes=64)
@@ -163,7 +178,7 @@ def tile_attend_bias_gate_topk_kernel(tc, qT, k_words, k_scales, vT, vs, kb, og,
             v_bf[:].bitcast(F32).rearrange("s (e u) -> s e u", u=2), v_turned[:].rearrange("s u e -> s e u")
         )
         v_codes = sb.tile([P, DV], U32, name="v_codes", align_bytes=64)
-        v_scale = shared.tile([P, DV], U8, name="v_scale", offset=3072, align_bytes=64)
+        v_scale = shared.tile([P, DV], U8, name="v_scale", offset=V_SCALE_AT, align_bytes=64)
 
         p_cols = []
         for b in range(QBLOCKS):

@@ -28,14 +28,17 @@ QBLOCKS = NQ // P
 ROW = P - 1
 
 WIDE_CHUNKS = 2
-EARLY = 320
+EARLY = 192
+MIDDLE = 128
+LATE_AT = EARLY + MIDDLE
 
 ROW_BYTES = 4 * SLOTS
 KEYS_AT = 0
-BIAS_ROW_AT = ROW_BYTES // 2
-VS_ROW_AT = ROW_BYTES
-V_SCALE_AT = BIAS_ROW_AT + ROW_BYTES
-QUERIES_AT = 2 * ROW_BYTES
+Q_CODES_AT = ROW_BYTES
+VS_ROW_AT = Q_CODES_AT + 4 * NQ
+BIAS_ROW_AT = VS_ROW_AT + 64 - ROW_BYTES
+V_SCALE_AT = VS_ROW_AT + 64
+QUERIES_AT = VS_ROW_AT + ROW_BYTES
 
 FLOPS = 2 * NQ * SLOTS * D + 2 * NQ * SLOTS * DV
 
@@ -82,17 +85,17 @@ def tile_attend_bias_gate_topk_kernel(tc, qT, k_words, k_scales, vT, vs, kb, og,
         og_sb = sb.tile([P, QBLOCKS, DV], F32, name="og_sb", tag="ks_pool", align_bytes=64)
         nc.sync.dma_start(og_sb[:], og[0].rearrange("(b q) e -> q b e", q=P))
 
-        q_bf = sb.tile([P, NQ, PACK], BF16, name="q_bf", align_bytes=64)
+        v_picked = sb.tile([P, EARLY + NQ * PACK], BF16, name="v_picked", align_bytes=64)
+        q_bf = v_picked[:, EARLY:]
         nc.scalar.copy(
-            q_bf[:].rearrange("p (c i) t -> p c t i", i=LINE), q_raw[:].rearrange("p t (c i) -> p c t i", i=LINE)
+            q_bf.rearrange("p (c i t) -> p c t i", i=LINE, t=PACK), q_raw[:].rearrange("p t (c i) -> p c t i", i=LINE)
         )
-        q_codes = sb.tile([P, NQ], U32, name="q_codes", align_bytes=64)
+        q_codes = shared.tile([P, NQ], U32, name="q_codes", offset=Q_CODES_AT, align_bytes=64)
         q_scale = sb.tile([P, NQ], U8, name="q_scale", align_bytes=64)
-        nc.vector.quantize_mx(q_codes[:].bitcast(FP8X4), q_scale[:], q_bf[:].rearrange("p q t -> p (q t)"))
+        nc.vector.quantize_mx(q_codes[:].bitcast(FP8X4), q_scale[:], q_bf)
 
         v_pool = sb.tile([P, POOL], BF16, name="v_pool", align_bytes=64)
         nc.scalar.activation(v_pool[:], v_raw[:], ACT.Copy)
-        v_picked = sb.tile([P, EARLY + 2 * P], BF16, name="v_picked", align_bytes=64)
         nc.scalar.activation(v_picked[:, :EARLY], v_pool[:].indirect(offsets[:, : EARLY // GROUP]), ACT.Copy)
 
         kb_turned = ps.tile([P, CHUNKS, P], F32, name="kb_turned", tag="col0")
@@ -139,19 +142,22 @@ def tile_attend_bias_gate_topk_kernel(tc, qT, k_words, k_scales, vT, vs, kb, og,
             for c in range(CHUNKS):
                 if c >= WIDE_CHUNKS:
                     if (c, b) == (WIDE_CHUNKS, 0):
-                        biased[c, b] = v_picked[:, EARLY:].bitcast(F32)
+                        biased[c, b] = v_picked[:, LATE_AT : LATE_AT + 2 * P].bitcast(F32)
                     else:
                         biased[c, b] = sb.tile([P, P], F32, name="biased%d_%d" % (c, b), align_bytes=64)[:]
                     nc.scalar.activation(biased[c, b], in_psum[c, b], ACT.Identity, bias=kb_col[:, c : c + 1])
                 nc.tensor.transpose(s_row[:, c * P : (c + 1) * P], biased[c, b], ident[:])
             s_rows.append(s_row)
 
-        nc.scalar.activation(v_picked[:, EARLY:SLOTS], v_pool[:].indirect(offsets[:, EARLY // GROUP :]), ACT.Copy)
+        nc.scalar.activation(v_picked[:, LATE_AT:SLOTS], v_pool[:].indirect(offsets[:, LATE_AT // GROUP :]), ACT.Copy)
 
         vs_row = shared.tile([P, SLOTS], F32, name="vs_row", offset=VS_ROW_AT, align_bytes=64)
         nc.vector.tensor_copy(vs_row[:], vs_pool[:].indirect(offsets[:]))
         vs_col = sb.tile([P, PACK], F32, name="vs_col", tag="vs_col")
         nc.sync.dma_start(vs_col[:], vs_row[ROW:P, :].rearrange("o (s t) -> o s t", t=PACK))
+        nc.vector.tensor_copy(
+            v_picked[:, EARLY:LATE_AT], v_raw[:].indirect(offsets[:, EARLY // GROUP : LATE_AT // GROUP])
+        )
 
         neg_max = [sb.tile([P, 1], F32, name="neg_max%d" % b) for b in range(QBLOCKS)]
         part_total = sb.tile([P, 2, QBLOCKS], F32, name="part_total")

@@ -27,18 +27,15 @@ CHUNKS = SLOTS // P
 QBLOCKS = NQ // P
 ROW = P - 1
 
-WIDE_CHUNKS = 2
-EARLY = 192
-MIDDLE = 128
-LATE_AT = EARLY + MIDDLE
+WIDE_CHUNKS = 3
+SCALAR_SLOTS = 288
+V_FIRST = 640
 
 ROW_BYTES = 4 * SLOTS
 KEYS_AT = 0
 Q_CODES_AT = ROW_BYTES
 VS_ROW_AT = Q_CODES_AT + 4 * NQ
 BIAS_ROW_AT = VS_ROW_AT + 64 - ROW_BYTES
-V_SCALE_AT = VS_ROW_AT + 64
-QUERIES_AT = VS_ROW_AT + ROW_BYTES
 
 FLOPS = 2 * NQ * SLOTS * D + 2 * NQ * SLOTS * DV
 
@@ -58,13 +55,12 @@ def tile_attend_bias_gate_topk_kernel(tc, qT, k_words, k_scales, vT, vs, kb, og,
         vs_pool = sb.tile([P, POOL], F32, name="vs_pool")
         nc.vector.memset(ks_pool[:].bitcast(I32), 0)
         nc.vector.memset(kb_pool[0:ROW, :], 0.0)
-        nc.vector.memset(vs_pool[:], 0.0)
         ident = sb.tile([P, P], F32, name="ident")
-        nc.vector.memset(ident[:], 0.0)
-        make_identity(nc, ident[:], nomemset=True)
+        make_identity(nc, ident[:])
+        nc.gpsimd.memset(vs_pool[0:ROW, :], 0.0)
 
         nc.scalar.dma_start(kb_pool[ROW:P, :], kb[0:1, :])
-        q_raw = shared.tile([P, PACK, NQ], F32, name="q_raw", offset=QUERIES_AT, align_bytes=64)
+        q_raw = sb.tile([P, PACK, NQ], F32, name="q_raw", align_bytes=64)
         nc.sync.dma_start(q_raw[:], qT[0].rearrange("(p t) q -> p t q", t=PACK))
         scale_rows = k_scales[0].rearrange("(a r) n -> r a n", r=PACK)
         for r in range(PACK):
@@ -72,10 +68,11 @@ def tile_attend_bias_gate_topk_kernel(tc, qT, k_words, k_scales, vT, vs, kb, og,
             queue.dma_start(ks_pool[r:P:QUADRANT, :].bitcast(I32), scale_rows[r].bitcast(I32))
 
         v_raw = sb.tile([P, POOL], F32, name="v_raw")
-        nc.sync.dma_start(v_raw[:], vT)
+        nc.sync.dma_start(v_raw[:, :V_FIRST], vT[:, :V_FIRST])
         kw_pool = sb.tile([P, POOL], I32, name="kw_pool", align_bytes=64)
         nc.sync.dma_start(kw_pool[:], k_words[0].rearrange("p n t -> p (n t)").bitcast(I32))
         nc.sync.dma_start(vs_pool[ROW:P, :], vs[0:1, :])
+        nc.sync.dma_start(v_raw[:, V_FIRST:], vT[:, V_FIRST:])
 
         kb_row = shared.tile([P, SLOTS], F32, name="kb_row", offset=BIAS_ROW_AT, align_bytes=64)
         nc.vector.tensor_copy(kb_row[:], kb_pool[:].indirect(offsets[:]))
@@ -85,8 +82,8 @@ def tile_attend_bias_gate_topk_kernel(tc, qT, k_words, k_scales, vT, vs, kb, og,
         og_sb = sb.tile([P, QBLOCKS, DV], F32, name="og_sb", tag="ks_pool", align_bytes=64)
         nc.sync.dma_start(og_sb[:], og[0].rearrange("(b q) e -> q b e", q=P))
 
-        v_picked = sb.tile([P, EARLY + NQ * PACK], BF16, name="v_picked", align_bytes=64)
-        q_bf = v_picked[:, EARLY:]
+        v_picked = sb.tile([P, SCALAR_SLOTS + NQ * PACK], BF16, name="v_picked", align_bytes=64)
+        q_bf = v_picked[:, SCALAR_SLOTS:]
         nc.scalar.copy(
             q_bf.rearrange("p (c i t) -> p c t i", i=LINE, t=PACK), q_raw[:].rearrange("p t (c i) -> p c t i", i=LINE)
         )
@@ -95,14 +92,14 @@ def tile_attend_bias_gate_topk_kernel(tc, qT, k_words, k_scales, vT, vs, kb, og,
         nc.vector.quantize_mx(q_codes[:].bitcast(FP8X4), q_scale[:], q_bf)
 
         v_pool = sb.tile([P, POOL], BF16, name="v_pool", align_bytes=64)
-        nc.scalar.activation(v_pool[:], v_raw[:], ACT.Copy)
-        nc.scalar.activation(v_picked[:, :EARLY], v_pool[:].indirect(offsets[:, : EARLY // GROUP]), ACT.Copy)
+        nc.scalar.activation(v_pool[:, :V_FIRST], v_raw[:, :V_FIRST], ACT.Copy)
+        nc.scalar.activation(v_pool[:, V_FIRST:], v_raw[:, V_FIRST:], ACT.Copy)
 
         kb_turned = ps.tile([P, CHUNKS, P], F32, name="kb_turned", tag="col0")
         for c in range(CHUNKS):
             nc.tensor.transpose(kb_turned[:, c, :], kb_row[:, c * P : (c + 1) * P], ident[:])
-        kb_col = shared.tile([P, CHUNKS], F32, name="kb_col", offset=QUERIES_AT, align_bytes=64)
-        nc.scalar.copy(kb_col[:], kb_turned[:, :, ROW])
+        kb_col = v_picked[:, : 2 * CHUNKS].bitcast(F32)
+        nc.scalar.copy(kb_col, kb_turned[:, :, ROW])
 
         k_picked = shared.tile([P, SLOTS], U32, name="k_picked", offset=KEYS_AT, align_bytes=64)
         in_psum, biased = {}, {}
@@ -141,22 +138,21 @@ def tile_attend_bias_gate_topk_kernel(tc, qT, k_words, k_scales, vT, vs, kb, og,
             s_row = ps.tile([P, SLOTS], F32, name="s_row%d" % b, tag=tag)
             for c in range(CHUNKS):
                 if c >= WIDE_CHUNKS:
-                    if (c, b) == (WIDE_CHUNKS, 0):
-                        biased[c, b] = v_picked[:, LATE_AT : LATE_AT + 2 * P].bitcast(F32)
-                    else:
-                        biased[c, b] = sb.tile([P, P], F32, name="biased%d_%d" % (c, b), align_bytes=64)[:]
+                    biased[c, b] = sb.tile([P, P], F32, name="biased%d" % b, tag="biased%d" % b, align_bytes=64)[:]
                     nc.scalar.activation(biased[c, b], in_psum[c, b], ACT.Identity, bias=kb_col[:, c : c + 1])
                 nc.tensor.transpose(s_row[:, c * P : (c + 1) * P], biased[c, b], ident[:])
             s_rows.append(s_row)
 
-        nc.scalar.activation(v_picked[:, LATE_AT:SLOTS], v_pool[:].indirect(offsets[:, LATE_AT // GROUP :]), ACT.Copy)
+        nc.scalar.activation(
+            v_picked[:, :SCALAR_SLOTS], v_pool[:].indirect(offsets[:, : SCALAR_SLOTS // GROUP]), ACT.Copy
+        )
 
         vs_row = shared.tile([P, SLOTS], F32, name="vs_row", offset=VS_ROW_AT, align_bytes=64)
         nc.vector.tensor_copy(vs_row[:], vs_pool[:].indirect(offsets[:]))
         vs_col = sb.tile([P, PACK], F32, name="vs_col", tag="vs_col")
         nc.sync.dma_start(vs_col[:], vs_row[ROW:P, :].rearrange("o (s t) -> o s t", t=PACK))
         nc.vector.tensor_copy(
-            v_picked[:, EARLY:LATE_AT], v_raw[:].indirect(offsets[:, EARLY // GROUP : LATE_AT // GROUP])
+            v_picked[:, SCALAR_SLOTS:SLOTS], v_raw[:].indirect(offsets[:, SCALAR_SLOTS // GROUP :])
         )
 
         neg_max = [sb.tile([P, 1], F32, name="neg_max%d" % b) for b in range(QBLOCKS)]
@@ -179,12 +175,13 @@ def tile_attend_bias_gate_topk_kernel(tc, qT, k_words, k_scales, vT, vs, kb, og,
         v_turned = ps.tile([P, 2, DV], F32, name="v_turned", tag=second_block_last_bank)
         for u in range(2):
             nc.tensor.transpose(v_turned[:, u, :], v_words[:, u : SLOTS // 2 : 2], ident[:])
-        v_bf = sb.tile([P, DV * PACK], BF16, name="v_bf", align_bytes=64)
+        v_bf = sb.tile([P, DV * PACK], BF16, name="v_bf", tag="biased1", align_bytes=64)
         nc.vector.tensor_copy(
             v_bf[:].bitcast(F32).rearrange("s (e u) -> s e u", u=2), v_turned[:].rearrange("s u e -> s e u")
         )
         v_codes = sb.tile([P, DV], U32, name="v_codes", align_bytes=64)
-        v_scale = shared.tile([P, DV], U8, name="v_scale", offset=V_SCALE_AT, align_bytes=64)
+        v_scale = sb.tile([P, DV], U8, name="v_scale", align_bytes=64)
+        nc.vector.quantize_mx(v_codes[:].bitcast(FP8X4), v_scale[:], v_bf[:])
 
         p_cols = []
         for b in range(QBLOCKS):
@@ -201,8 +198,6 @@ def tile_attend_bias_gate_topk_kernel(tc, qT, k_words, k_scales, vT, vs, kb, og,
                 vs_col[:].unsqueeze(1).to_broadcast([P, P, PACK]),
                 ALU.mult,
             )
-            if b == 0:
-                nc.vector.quantize_mx(v_codes[:].bitcast(FP8X4), v_scale[:], v_bf[:])
 
         half_tanh = sb.tile([P, QBLOCKS, DV], F32, name="half_tanh", tag="p_row0", align_bytes=64)
         nc.scalar.activation(half_tanh[:], og_sb[:], ACT.Tanh, scale=0.5)

@@ -29,7 +29,8 @@ ROW = P - 1
 
 WIDE_CHUNKS = 3
 SCALAR_SLOTS = 288
-V_FIRST = 640
+SCALAR_LINES = 48
+V_FIRST = 448
 
 ROW_BYTES = 4 * SLOTS
 KEYS_AT = 0
@@ -84,9 +85,10 @@ def tile_attend_bias_gate_topk_kernel(tc, qT, k_words, k_scales, vT, vs, kb, og,
 
         v_picked = sb.tile([P, SCALAR_SLOTS + NQ * PACK], BF16, name="v_picked", align_bytes=64)
         q_bf = v_picked[:, SCALAR_SLOTS:]
-        nc.scalar.copy(
-            q_bf.rearrange("p (c i t) -> p c t i", i=LINE, t=PACK), q_raw[:].rearrange("p t (c i) -> p c t i", i=LINE)
-        )
+        q_out = q_bf.rearrange("p (c i t) -> p c t i", i=LINE, t=PACK)
+        q_in = q_raw[:].rearrange("p t (c i) -> p c t i", i=LINE)
+        nc.scalar.copy(q_out[:, :SCALAR_LINES], q_in[:, :SCALAR_LINES])
+        nc.vector.tensor_copy(q_out[:, SCALAR_LINES:], q_in[:, SCALAR_LINES:])
         q_codes = shared.tile([P, NQ], U32, name="q_codes", offset=Q_CODES_AT, align_bytes=64)
         q_scale = sb.tile([P, NQ], U8, name="q_scale", align_bytes=64)
         nc.vector.quantize_mx(q_codes[:].bitcast(FP8X4), q_scale[:], q_bf)

@@ -57,16 +57,19 @@ def tile_attend_bias_gate_topk_kernel(tc, qT, k_words, k_scales, vT, vs, kb, og,
         nc.vector.memset(ks_pool[:].bitcast(I32), 0)
         nc.vector.memset(kb_pool[0:ROW, :], 0.0)
         ident = sb.tile([P, P], F32, name="ident")
-        make_identity(nc, ident[:])
-        nc.gpsimd.memset(vs_pool[0:ROW, :], 0.0)
+        nc.vector.memset(vs_pool[:], 0.0)
+        nc.vector.memset(ident[:], 0.0)
+        make_identity(nc, ident[:], nomemset=True)
 
         nc.scalar.dma_start(kb_pool[ROW:P, :], kb[0:1, :])
         q_raw = sb.tile([P, PACK, NQ], F32, name="q_raw", align_bytes=64)
         nc.sync.dma_start(q_raw[:], qT[0].rearrange("(p t) q -> p t q", t=PACK))
-        scale_rows = k_scales[0].rearrange("(a r) n -> r a n", r=PACK)
-        for r in range(PACK):
-            queue = nc.sync if r < PACK // 2 else nc.scalar
-            queue.dma_start(ks_pool[r:P:QUADRANT, :].bitcast(I32), scale_rows[r].bitcast(I32))
+        for a in range(P // QUADRANT):
+            queue = nc.sync if a < 2 else nc.scalar
+            queue.dma_start(
+                ks_pool[a * QUADRANT : a * QUADRANT + PACK, :].bitcast(I32),
+                k_scales[0, a * PACK : (a + 1) * PACK, :].bitcast(I32),
+            )
 
         v_raw = sb.tile([P, POOL], F32, name="v_raw")
         nc.sync.dma_start(v_raw[:, :V_FIRST], vT[:, :V_FIRST])

@@ -27,9 +27,10 @@ CHUNKS = SLOTS // P
 QBLOCKS = NQ // P
 ROW = P - 1
 
-WIDE_CHUNKS = 3
-SCALAR_SLOTS = 288
+WIDE_CHUNKS = 1
+SCALAR_SLOTS = 320
 SCALAR_LINES = 48
+LEAD = 32
 V_FIRST = 448
 
 ROW_BYTES = 4 * SLOTS
@@ -86,7 +87,8 @@ def tile_attend_bias_gate_topk_kernel(tc, qT, k_words, k_scales, vT, vs, kb, og,
         og_sb = sb.tile([P, QBLOCKS, DV], F32, name="og_sb", tag="ks_pool", align_bytes=64)
         nc.sync.dma_start(og_sb[:], og[0].rearrange("(b q) e -> q b e", q=P))
 
-        v_picked = sb.tile([P, SCALAR_SLOTS + NQ * PACK], BF16, name="v_picked", align_bytes=64)
+        staging = sb.tile([P, LEAD + SCALAR_SLOTS + NQ * PACK], BF16, name="staging", align_bytes=64)
+        v_picked = staging[:, LEAD:]
         q_bf = v_picked[:, SCALAR_SLOTS:]
         q_out = q_bf.rearrange("p (c i t) -> p c t i", i=LINE, t=PACK)
         q_in = q_raw[:].rearrange("p t (c i) -> p c t i", i=LINE)
@@ -102,9 +104,10 @@ def tile_attend_bias_gate_topk_kernel(tc, qT, k_words, k_scales, vT, vs, kb, og,
 
         kb_turned = ps.tile([P, CHUNKS, P], F32, name="kb_turned", tag="col0")
         for c in range(CHUNKS):
-            nc.tensor.transpose(kb_turned[:, c, :], kb_row[:, c * P : (c + 1) * P], ident[:])
-        kb_col = v_picked[:, : 2 * CHUNKS].bitcast(F32)
-        nc.scalar.copy(kb_col, kb_turned[:, :, ROW])
+            nc.tensor.transpose(kb_turned[:, CHUNKS - 1 - c, :], kb_row[:, c * P : (c + 1) * P], ident[:])
+        kb_cols = staging[:, LEAD - 2 : LEAD - 2 + 2 * CHUNKS].bitcast(F32)
+        nc.scalar.copy(kb_cols, kb_turned[:, :, ROW])
+        kb_col = [kb_cols[:, CHUNKS - 1 - c : CHUNKS - c] for c in range(CHUNKS)]
 
         k_picked = shared.tile([P, SLOTS], U32, name="k_picked", offset=KEYS_AT, align_bytes=64)
         in_psum, biased = {}, {}
@@ -129,7 +132,7 @@ def tile_attend_bias_gate_topk_kernel(tc, qT, k_words, k_scales, vT, vs, kb, og,
                 )
                 if c < WIDE_CHUNKS:
                     wide = sb.tile([P, NQ], F32, name="wide%d" % c, align_bytes=64)
-                    nc.scalar.activation(wide[:], scores[:], ACT.Identity, bias=kb_col[:, c : c + 1])
+                    nc.scalar.activation(wide[:], scores[:], ACT.Identity, bias=kb_col[c])
                     for b in range(QBLOCKS):
                         biased[c, b] = wide[:, b * P : (b + 1) * P]
                 else:
@@ -143,8 +146,8 @@ def tile_attend_bias_gate_topk_kernel(tc, qT, k_words, k_scales, vT, vs, kb, og,
             s_row = ps.tile([P, SLOTS], F32, name="s_row%d" % b, tag=tag)
             for c in range(CHUNKS):
                 if c >= WIDE_CHUNKS:
-                    biased[c, b] = sb.tile([P, P], F32, name="biased%d" % b, tag="biased%d" % b, align_bytes=64)[:]
-                    nc.scalar.activation(biased[c, b], in_psum[c, b], ACT.Identity, bias=kb_col[:, c : c + 1])
+                    biased[c, b] = sb.tile([P, P], F32, name="biased%d_%d" % (c, b), tag="biased%d_%d" % (c, b), align_bytes=64)[:]
+                    nc.scalar.activation(biased[c, b], in_psum[c, b], ACT.Identity, bias=kb_col[c])
                 nc.tensor.transpose(s_row[:, c * P : (c + 1) * P], biased[c, b], ident[:])
             s_rows.append(s_row)
 
@@ -176,11 +179,11 @@ def tile_attend_bias_gate_topk_kernel(tc, qT, k_words, k_scales, vT, vs, kb, og,
                 )
             p_rows.append(p_row)
 
-        v_words = v_picked[:].bitcast(F32)
+        v_words = v_picked.bitcast(F32)
         v_turned = ps.tile([P, 2, DV], F32, name="v_turned", tag=second_block_last_bank)
         for u in range(2):
             nc.tensor.transpose(v_turned[:, u, :], v_words[:, u : SLOTS // 2 : 2], ident[:])
-        v_bf = sb.tile([P, DV * PACK], BF16, name="v_bf", tag="biased1", align_bytes=64)
+        v_bf = sb.tile([P, DV * PACK], BF16, name="v_bf", tag="biased3_1", align_bytes=64)
         nc.vector.tensor_copy(
             v_bf[:].bitcast(F32).rearrange("s (e u) -> s e u", u=2), v_turned[:].rearrange("s u e -> s e u")
         )

@@ -27,16 +27,14 @@ CHUNKS = SLOTS // P
 QBLOCKS = NQ // P
 ROW = P - 1
 
-WIDE_CHUNKS = 1
-SCALAR_SLOTS = 320
-SCALAR_LINES = 48
+WIDE_CHUNKS = 2
+SCALAR_SLOTS = 352
 LEAD = 32
-V_FIRST = 448
 
 ROW_BYTES = 4 * SLOTS
 KEYS_AT = 0
-Q_CODES_AT = ROW_BYTES
-VS_ROW_AT = Q_CODES_AT + 4 * NQ
+STAGING_AT = ROW_BYTES
+VS_ROW_AT = STAGING_AT + 2 * (LEAD + SLOTS)
 BIAS_ROW_AT = VS_ROW_AT + 64 - ROW_BYTES
 
 FLOPS = 2 * NQ * SLOTS * D + 2 * NQ * SLOTS * DV
@@ -71,13 +69,11 @@ def tile_attend_bias_gate_topk_kernel(tc, qT, k_words, k_scales, vT, vs, kb, og,
                 ks_pool[a * QUADRANT : a * QUADRANT + PACK, :].bitcast(I32),
                 k_scales[0, a * PACK : (a + 1) * PACK, :].bitcast(I32),
             )
-
-        v_raw = sb.tile([P, POOL], F32, name="v_raw")
-        nc.sync.dma_start(v_raw[:, :V_FIRST], vT[:, :V_FIRST])
         kw_pool = sb.tile([P, POOL], I32, name="kw_pool", align_bytes=64)
         nc.sync.dma_start(kw_pool[:], k_words[0].rearrange("p n t -> p (n t)").bitcast(I32))
+        v_pool = sb.tile([P, POOL], F32, name="v_pool")
+        nc.sync.dma_start(v_pool[:], vT)
         nc.sync.dma_start(vs_pool[ROW:P, :], vs[0:1, :])
-        nc.sync.dma_start(v_raw[:, V_FIRST:], vT[:, V_FIRST:])
 
         kb_row = shared.tile([P, SLOTS], F32, name="kb_row", offset=BIAS_ROW_AT, align_bytes=64)
         nc.vector.tensor_copy(kb_row[:], kb_pool[:].indirect(offsets[:]))
@@ -87,20 +83,15 @@ def tile_attend_bias_gate_topk_kernel(tc, qT, k_words, k_scales, vT, vs, kb, og,
         og_sb = sb.tile([P, QBLOCKS, DV], F32, name="og_sb", tag="ks_pool", align_bytes=64)
         nc.sync.dma_start(og_sb[:], og[0].rearrange("(b q) e -> q b e", q=P))
 
-        staging = sb.tile([P, LEAD + SCALAR_SLOTS + NQ * PACK], BF16, name="staging", align_bytes=64)
+        staging = shared.tile([P, LEAD + SLOTS], BF16, name="staging", offset=STAGING_AT, align_bytes=64)
         v_picked = staging[:, LEAD:]
-        q_bf = v_picked[:, SCALAR_SLOTS:]
-        q_out = q_bf.rearrange("p (c i t) -> p c t i", i=LINE, t=PACK)
+        q_bf = sb.tile([P, NQ * PACK], BF16, name="q_bf", align_bytes=64)
+        q_out = q_bf[:].rearrange("p (c i t) -> p c t i", i=LINE, t=PACK)
         q_in = q_raw[:].rearrange("p t (c i) -> p c t i", i=LINE)
-        nc.scalar.copy(q_out[:, :SCALAR_LINES], q_in[:, :SCALAR_LINES])
-        nc.vector.tensor_copy(q_out[:, SCALAR_LINES:], q_in[:, SCALAR_LINES:])
-        q_codes = shared.tile([P, NQ], U32, name="q_codes", offset=Q_CODES_AT, align_bytes=64)
+        nc.scalar.copy(q_out, q_in)
+        q_codes = sb.tile([P, NQ], U32, name="q_codes", align_bytes=64)
         q_scale = sb.tile([P, NQ], U8, name="q_scale", align_bytes=64)
-        nc.vector.quantize_mx(q_codes[:].bitcast(FP8X4), q_scale[:], q_bf)
-
-        v_pool = sb.tile([P, POOL], BF16, name="v_pool", align_bytes=64)
-        nc.scalar.activation(v_pool[:, :V_FIRST], v_raw[:, :V_FIRST], ACT.Copy)
-        nc.scalar.activation(v_pool[:, V_FIRST:], v_raw[:, V_FIRST:], ACT.Copy)
+        nc.vector.quantize_mx(q_codes[:].bitcast(FP8X4), q_scale[:], q_bf[:])
 
         kb_turned = ps.tile([P, CHUNKS, P], F32, name="kb_turned", tag="col0")
         for c in range(CHUNKS):
@@ -160,7 +151,7 @@ def tile_attend_bias_gate_topk_kernel(tc, qT, k_words, k_scales, vT, vs, kb, og,
         vs_col = sb.tile([P, PACK], F32, name="vs_col", tag="vs_col")
         nc.sync.dma_start(vs_col[:], vs_row[ROW:P, :].rearrange("o (s t) -> o s t", t=PACK))
         nc.vector.tensor_copy(
-            v_picked[:, SCALAR_SLOTS:SLOTS], v_raw[:].indirect(offsets[:, SCALAR_SLOTS // GROUP :])
+            v_picked[:, SCALAR_SLOTS:SLOTS], v_pool[:].indirect(offsets[:, SCALAR_SLOTS // GROUP :])
         )
 
         neg_max = [sb.tile([P, 1], F32, name="neg_max%d" % b) for b in range(QBLOCKS)]

@@ -27,15 +27,13 @@ CHUNKS = SLOTS // P
 QBLOCKS = NQ // P
 ROW = P - 1
 
-WIDE_CHUNKS = 2
-SCALAR_SLOTS = 352
-LEAD = 32
+WIDE_CHUNKS = 0
+SCALAR_LINES = 48
 
-ROW_BYTES = 4 * SLOTS
 KEYS_AT = 0
-STAGING_AT = ROW_BYTES
-VS_ROW_AT = STAGING_AT + 2 * (LEAD + SLOTS)
-BIAS_ROW_AT = VS_ROW_AT + 64 - ROW_BYTES
+Q_CODES_AT = 4 * SLOTS
+VALUES_AT = Q_CODES_AT + 4 * NQ
+BIAS_ROW_AT = VALUES_AT + 64 - 4 * SLOTS
 
 FLOPS = 2 * NQ * SLOTS * D + 2 * NQ * SLOTS * DV
 
@@ -50,13 +48,16 @@ def tile_attend_bias_gate_topk_kernel(tc, qT, k_words, k_scales, vT, vs, kb, og,
         offsets = sb.tile([P, SLOTS // GROUP], U16, name="offsets")
         nc.sync.dma_start(offsets[:], offs)
 
+        def listed(pool, first, last):
+            return pool.indirect(offsets[:, first // GROUP : last // GROUP])
+
         ks_pool = sb.tile([P, POOL], U8, name="ks_pool", tag="ks_pool", align_bytes=64)
-        kb_pool = sb.tile([P, POOL], F32, name="kb_pool")
+        kb_pool = sb.tile([P, POOL], F32, name="kb_pool", tag="kb_pool", align_bytes=64)
         vs_pool = sb.tile([P, POOL], F32, name="vs_pool")
+        ident = sb.tile([P, P], F32, name="ident")
         nc.vector.memset(ks_pool[:].bitcast(I32), 0)
         nc.vector.memset(kb_pool[0:ROW, :], 0.0)
-        ident = sb.tile([P, P], F32, name="ident")
-        nc.vector.memset(vs_pool[:], 0.0)
+        nc.vector.memset(vs_pool[0:ROW, :], 0.0)
         nc.vector.memset(ident[:], 0.0)
         make_identity(nc, ident[:], nomemset=True)
 
@@ -69,45 +70,47 @@ def tile_attend_bias_gate_topk_kernel(tc, qT, k_words, k_scales, vT, vs, kb, og,
                 ks_pool[a * QUADRANT : a * QUADRANT + PACK, :].bitcast(I32),
                 k_scales[0, a * PACK : (a + 1) * PACK, :].bitcast(I32),
             )
+        nc.sync.dma_start(vs_pool[ROW:P, :], vs[0:1, :])
         kw_pool = sb.tile([P, POOL], I32, name="kw_pool", align_bytes=64)
         nc.sync.dma_start(kw_pool[:], k_words[0].rearrange("p n t -> p (n t)").bitcast(I32))
-        v_pool = sb.tile([P, POOL], F32, name="v_pool")
+        v_pool = sb.tile([P, POOL], F32, name="v_pool", tag="v_pool")
         nc.sync.dma_start(v_pool[:], vT)
-        nc.sync.dma_start(vs_pool[ROW:P, :], vs[0:1, :])
 
         kb_row = shared.tile([P, SLOTS], F32, name="kb_row", offset=BIAS_ROW_AT, align_bytes=64)
-        nc.vector.tensor_copy(kb_row[:], kb_pool[:].indirect(offsets[:]))
+        nc.vector.tensor_copy(kb_row[:], listed(kb_pool[:], 0, SLOTS))
         k_scale = sb.tile([P, SLOTS], U8, name="k_scale", align_bytes=64)
-        nc.vector.tensor_copy(k_scale[:], ks_pool[:].indirect(offsets[:]))
+        nc.vector.tensor_copy(k_scale[:], listed(ks_pool[:], 0, SLOTS))
 
         og_sb = sb.tile([P, QBLOCKS, DV], F32, name="og_sb", tag="ks_pool", align_bytes=64)
         nc.sync.dma_start(og_sb[:], og[0].rearrange("(b q) e -> q b e", q=P))
 
-        staging = shared.tile([P, LEAD + SLOTS], BF16, name="staging", offset=STAGING_AT, align_bytes=64)
-        v_picked = staging[:, LEAD:]
         q_bf = sb.tile([P, NQ * PACK], BF16, name="q_bf", align_bytes=64)
         q_out = q_bf[:].rearrange("p (c i t) -> p c t i", i=LINE, t=PACK)
         q_in = q_raw[:].rearrange("p t (c i) -> p c t i", i=LINE)
-        nc.scalar.copy(q_out, q_in)
-        q_codes = sb.tile([P, NQ], U32, name="q_codes", align_bytes=64)
+        nc.scalar.copy(q_out[:, :SCALAR_LINES], q_in[:, :SCALAR_LINES])
+        nc.vector.tensor_copy(q_out[:, SCALAR_LINES:], q_in[:, SCALAR_LINES:])
+        q_codes = shared.tile([P, NQ], U32, name="q_codes", offset=Q_CODES_AT, align_bytes=64)
         q_scale = sb.tile([P, NQ], U8, name="q_scale", align_bytes=64)
         nc.vector.quantize_mx(q_codes[:].bitcast(FP8X4), q_scale[:], q_bf[:])
 
+        vs_row = sb.tile([P, SLOTS], F32, name="vs_row", align_bytes=64)
+        nc.scalar.activation(vs_row[:], listed(vs_pool[:], 0, SLOTS), ACT.Copy)
+        vs_col = sb.tile([P, PACK], F32, name="vs_col", tag="vs_col")
+        nc.sync.dma_start(vs_col[:], vs_row[ROW:P, :].rearrange("o (s t) -> o s t", t=PACK))
+
         kb_turned = ps.tile([P, CHUNKS, P], F32, name="kb_turned", tag="col0")
         for c in range(CHUNKS):
-            nc.tensor.transpose(kb_turned[:, CHUNKS - 1 - c, :], kb_row[:, c * P : (c + 1) * P], ident[:])
-        kb_cols = staging[:, LEAD - 2 : LEAD - 2 + 2 * CHUNKS].bitcast(F32)
-        nc.scalar.copy(kb_cols, kb_turned[:, :, ROW])
-        kb_col = [kb_cols[:, CHUNKS - 1 - c : CHUNKS - c] for c in range(CHUNKS)]
+            nc.tensor.transpose(kb_turned[:, c, :], kb_row[:, c * P : (c + 1) * P], ident[:])
+        kb_cols = sb.tile([P, CHUNKS], F32, name="kb_cols")
+        nc.scalar.copy(kb_cols[:], kb_turned[:, :, ROW])
+        kb_col = [kb_cols[:, c : c + 1] for c in range(CHUNKS)]
 
         k_picked = shared.tile([P, SLOTS], U32, name="k_picked", offset=KEYS_AT, align_bytes=64)
         in_psum, biased = {}, {}
         for c in range(CHUNKS):
             cols = slice(c * P, (c + 1) * P)
             k_codes = k_picked[:, cols]
-            nc.vector.tensor_copy(
-                k_codes, kw_pool[:].bitcast(U32).indirect(offsets[:, c * P // GROUP : (c + 1) * P // GROUP])
-            )
+            nc.vector.tensor_copy(k_codes, listed(kw_pool[:].bitcast(U32), c * P, (c + 1) * P))
             width = NQ if c < CHUNKS - 1 else P
             for q0 in range(0, NQ, width):
                 label = "%d_%d" % (c, q0)
@@ -130,6 +133,9 @@ def tile_attend_bias_gate_topk_kernel(tc, qT, k_words, k_scales, vT, vs, kb, og,
                     for b in range(q0 // P, (q0 + width) // P):
                         in_psum[c, b] = scores[:, b * P - q0 : (b + 1) * P - q0]
 
+        v_picked = shared.tile([P, SLOTS], BF16, name="v_picked", offset=VALUES_AT, align_bytes=64)
+        nc.vector.tensor_copy(v_picked[:], listed(v_pool[:], 0, SLOTS))
+
         first_block_last_bank = "sc%d_%d" % (CHUNKS - 1, 0)
         second_block_last_bank = "sc%d_%d" % (CHUNKS - 1, P)
         s_rows = []
@@ -141,18 +147,6 @@ def tile_attend_bias_gate_topk_kernel(tc, qT, k_words, k_scales, vT, vs, kb, og,
                     nc.scalar.activation(biased[c, b], in_psum[c, b], ACT.Identity, bias=kb_col[c])
                 nc.tensor.transpose(s_row[:, c * P : (c + 1) * P], biased[c, b], ident[:])
             s_rows.append(s_row)
-
-        nc.scalar.activation(
-            v_picked[:, :SCALAR_SLOTS], v_pool[:].indirect(offsets[:, : SCALAR_SLOTS // GROUP]), ACT.Copy
-        )
-
-        vs_row = shared.tile([P, SLOTS], F32, name="vs_row", offset=VS_ROW_AT, align_bytes=64)
-        nc.vector.tensor_copy(vs_row[:], vs_pool[:].indirect(offsets[:]))
-        vs_col = sb.tile([P, PACK], F32, name="vs_col", tag="vs_col")
-        nc.sync.dma_start(vs_col[:], vs_row[ROW:P, :].rearrange("o (s t) -> o s t", t=PACK))
-        nc.vector.tensor_copy(
-            v_picked[:, SCALAR_SLOTS:SLOTS], v_pool[:].indirect(offsets[:, SCALAR_SLOTS // GROUP :])
-        )
 
         neg_max = [sb.tile([P, 1], F32, name="neg_max%d" % b) for b in range(QBLOCKS)]
         part_total = sb.tile([P, 2, QBLOCKS], F32, name="part_total")
@@ -170,7 +164,7 @@ def tile_attend_bias_gate_topk_kernel(tc, qT, k_words, k_scales, vT, vs, kb, og,
                 )
             p_rows.append(p_row)
 
-        v_words = v_picked.bitcast(F32)
+        v_words = v_picked[:].bitcast(F32)
         v_turned = ps.tile([P, 2, DV], F32, name="v_turned", tag=second_block_last_bank)
         for u in range(2):
             nc.tensor.transpose(v_turned[:, u, :], v_words[:, u : SLOTS // 2 : 2], ident[:])

@@ -29,6 +29,8 @@ ROW = P - 1
 
 WIDE_CHUNKS = 0
 SCALAR_LINES = 48
+V_SCALAR = 160
+LEAD = 32
 
 KEYS_AT = 0
 Q_CODES_AT = 4 * SLOTS
@@ -100,10 +102,12 @@ def tile_attend_bias_gate_topk_kernel(tc, qT, k_words, k_scales, vT, vs, kb, og,
 
         kb_turned = ps.tile([P, CHUNKS, P], F32, name="kb_turned", tag="col0")
         for c in range(CHUNKS):
-            nc.tensor.transpose(kb_turned[:, c, :], kb_row[:, c * P : (c + 1) * P], ident[:])
-        kb_cols = sb.tile([P, CHUNKS], F32, name="kb_cols")
-        nc.scalar.copy(kb_cols[:], kb_turned[:, :, ROW])
-        kb_col = [kb_cols[:, c : c + 1] for c in range(CHUNKS)]
+            nc.tensor.transpose(kb_turned[:, CHUNKS - 1 - c, :], kb_row[:, c * P : (c + 1) * P], ident[:])
+        staging = shared.tile([P, LEAD + SLOTS], BF16, name="staging", offset=VALUES_AT, align_bytes=64)
+        v_picked = staging[:, LEAD:]
+        kb_cols = staging[:, LEAD - 2 : LEAD - 2 + 2 * CHUNKS].bitcast(F32)
+        nc.scalar.copy(kb_cols, kb_turned[:, :, ROW])
+        kb_col = [kb_cols[:, CHUNKS - 1 - c : CHUNKS - c] for c in range(CHUNKS)]
 
         k_picked = shared.tile([P, SLOTS], U32, name="k_picked", offset=KEYS_AT, align_bytes=64)
         in_psum, biased = {}, {}
@@ -133,8 +137,7 @@ def tile_attend_bias_gate_topk_kernel(tc, qT, k_words, k_scales, vT, vs, kb, og,
                     for b in range(q0 // P, (q0 + width) // P):
                         in_psum[c, b] = scores[:, b * P - q0 : (b + 1) * P - q0]
 
-        v_picked = shared.tile([P, SLOTS], BF16, name="v_picked", offset=VALUES_AT, align_bytes=64)
-        nc.vector.tensor_copy(v_picked[:], listed(v_pool[:], 0, SLOTS))
+        nc.vector.tensor_copy(v_picked[:, V_SCALAR:], listed(v_pool[:], V_SCALAR, SLOTS))
 
         first_block_last_bank = "sc%d_%d" % (CHUNKS - 1, 0)
         second_block_last_bank = "sc%d_%d" % (CHUNKS - 1, P)
@@ -147,6 +150,8 @@ def tile_attend_bias_gate_topk_kernel(tc, qT, k_words, k_scales, vT, vs, kb, og,
                     nc.scalar.activation(biased[c, b], in_psum[c, b], ACT.Identity, bias=kb_col[c])
                 nc.tensor.transpose(s_row[:, c * P : (c + 1) * P], biased[c, b], ident[:])
             s_rows.append(s_row)
+
+        nc.scalar.activation(v_picked[:, :V_SCALAR], listed(v_pool[:], 0, V_SCALAR), ACT.Copy)
 
         neg_max = [sb.tile([P, 1], F32, name="neg_max%d" % b) for b in range(QBLOCKS)]
         part_total = sb.tile([P, 2, QBLOCKS], F32, name="part_total")
@@ -164,7 +169,7 @@ def tile_attend_bias_gate_topk_kernel(tc, qT, k_words, k_scales, vT, vs, kb, og,
                 )
             p_rows.append(p_row)
 
-        v_words = v_picked[:].bitcast(F32)
+        v_words = v_picked.bitcast(F32)
         v_turned = ps.tile([P, 2, DV], F32, name="v_turned", tag=second_block_last_bank)
         for u in range(2):
             nc.tensor.transpose(v_turned[:, u, :], v_words[:, u : SLOTS // 2 : 2], ident[:])

@@ -31,11 +31,12 @@ WIDE_CHUNKS = 0
 SCALAR_LINES = 48
 V_SCALAR = 160
 LEAD = 32
+LAST = SLOTS - P
 
 KEYS_AT = 0
-Q_CODES_AT = 4 * SLOTS
-VALUES_AT = Q_CODES_AT + 4 * NQ
-BIAS_ROW_AT = VALUES_AT + 64 - 4 * SLOTS
+Q_SCALE_AT = 4 * SLOTS
+VALUES_AT = Q_SCALE_AT + NQ
+BIAS_ROW_AT = Q_SCALE_AT - 64
 
 FLOPS = 2 * NQ * SLOTS * D + 2 * NQ * SLOTS * DV
 
@@ -78,8 +79,15 @@ def tile_attend_bias_gate_topk_kernel(tc, qT, k_words, k_scales, vT, vs, kb, og,
         v_pool = sb.tile([P, POOL], F32, name="v_pool", tag="v_pool")
         nc.sync.dma_start(v_pool[:], vT)
 
-        kb_row = shared.tile([P, SLOTS], F32, name="kb_row", offset=BIAS_ROW_AT, align_bytes=64)
-        nc.vector.tensor_copy(kb_row[:], listed(kb_pool[:], 0, SLOTS))
+        kb_front = shared.tile([P, LAST], F32, name="kb_front", offset=BIAS_ROW_AT, align_bytes=64)
+        vs_row = sb.tile([P, SLOTS], F32, name="vs_row", align_bytes=64)
+        kb_last = vs_row[:, LAST:]
+        nc.vector.tensor_copy(kb_front[:], listed(kb_pool[:], 0, LAST))
+        nc.vector.tensor_copy(kb_last, listed(kb_pool[:], LAST, SLOTS))
+        kb_chunks = [kb_front[:, c * P : (c + 1) * P] for c in range(CHUNKS - 1)] + [kb_last]
+        kb_turned = ps.tile([P, CHUNKS, P], F32, name="kb_turned", tag="col0")
+        for c in range(CHUNKS):
+            nc.tensor.transpose(kb_turned[:, CHUNKS - 1 - c, :], kb_chunks[c], ident[:])
         k_scale = sb.tile([P, SLOTS], U8, name="k_scale", align_bytes=64)
         nc.vector.tensor_copy(k_scale[:], listed(ks_pool[:], 0, SLOTS))
 
@@ -91,18 +99,12 @@ def tile_attend_bias_gate_topk_kernel(tc, qT, k_words, k_scales, vT, vs, kb, og,
         q_in = q_raw[:].rearrange("p t (c i) -> p c t i", i=LINE)
         nc.scalar.copy(q_out[:, :SCALAR_LINES], q_in[:, :SCALAR_LINES])
         nc.vector.tensor_copy(q_out[:, SCALAR_LINES:], q_in[:, SCALAR_LINES:])
-        q_codes = shared.tile([P, NQ], U32, name="q_codes", offset=Q_CODES_AT, align_bytes=64)
-        q_scale = sb.tile([P, NQ], U8, name="q_scale", align_bytes=64)
+        q_codes = sb.tile([P, NQ], U32, name="q_codes", align_bytes=64)
+        q_scale = shared.tile([P, NQ], U8, name="q_scale", offset=Q_SCALE_AT, align_bytes=64)
         nc.vector.quantize_mx(q_codes[:].bitcast(FP8X4), q_scale[:], q_bf[:])
 
-        vs_row = sb.tile([P, SLOTS], F32, name="vs_row", align_bytes=64)
-        nc.scalar.activation(vs_row[:], listed(vs_pool[:], 0, SLOTS), ACT.Copy)
-        vs_col = sb.tile([P, PACK], F32, name="vs_col", tag="vs_col")
-        nc.sync.dma_start(vs_col[:], vs_row[ROW:P, :].rearrange("o (s t) -> o s t", t=PACK))
+        nc.scalar.activation(vs_row[:, :LAST], listed(vs_pool[:], 0, LAST), ACT.Copy)
 
-        kb_turned = ps.tile([P, CHUNKS, P], F32, name="kb_turned", tag="col0")
-        for c in range(CHUNKS):
-            nc.tensor.transpose(kb_turned[:, CHUNKS - 1 - c, :], kb_row[:, c * P : (c + 1) * P], ident[:])
         staging = shared.tile([P, LEAD + SLOTS], BF16, name="staging", offset=VALUES_AT, align_bytes=64)
         v_picked = staging[:, LEAD:]
         kb_cols = staging[:, LEAD - 2 : LEAD - 2 + 2 * CHUNKS].bitcast(F32)
@@ -137,6 +139,9 @@ def tile_attend_bias_gate_topk_kernel(tc, qT, k_words, k_scales, vT, vs, kb, og,
                     for b in range(q0 // P, (q0 + width) // P):
                         in_psum[c, b] = scores[:, b * P - q0 : (b + 1) * P - q0]
 
+        nc.vector.tensor_copy(vs_row[:, LAST:], listed(vs_pool[:], LAST, SLOTS))
+        vs_col = sb.tile([P, PACK], F32, name="vs_col", tag="vs_col")
+        nc.sync.dma_start(vs_col[:], vs_row[ROW:P, :].rearrange("o (s t) -> o s t", t=PACK))
         nc.vector.tensor_copy(v_picked[:, V_SCALAR:], listed(v_pool[:], V_SCALAR, SLOTS))
 
         first_block_last_bank = "sc%d_%d" % (CHUNKS - 1, 0)

@@ -68,14 +68,13 @@ def tile_attend_bias_gate_topk_kernel(tc, qT, k_words, k_scales, vT, vs, kb, og,
         q_raw = sb.tile([P, PACK, NQ], F32, name="q_raw", align_bytes=64)
         nc.sync.dma_start(q_raw[:], qT[0].rearrange("(p t) q -> p t q", t=PACK))
         for a in range(P // QUADRANT):
-            queue = nc.sync if a < 2 else nc.scalar
-            queue.dma_start(
+            nc.sync.dma_start(
                 ks_pool[a * QUADRANT : a * QUADRANT + PACK, :].bitcast(I32),
                 k_scales[0, a * PACK : (a + 1) * PACK, :].bitcast(I32),
             )
-        nc.sync.dma_start(vs_pool[ROW:P, :], vs[0:1, :])
         kw_pool = sb.tile([P, POOL], I32, name="kw_pool", align_bytes=64)
         nc.sync.dma_start(kw_pool[:], k_words[0].rearrange("p n t -> p (n t)").bitcast(I32))
+        nc.sync.dma_start(vs_pool[ROW:P, :], vs[0:1, :])
         v_pool = sb.tile([P, POOL], F32, name="v_pool", tag="v_pool")
         nc.sync.dma_start(v_pool[:], vT)
 

@@ -28,9 +28,10 @@ QBLOCKS = NQ // P
 ROW = P - 1
 
 WIDE_CHUNKS = 0
-SCALAR_LINES = 48
+SCALAR_LINES = 56
 V_SCALAR = 160
 LEAD = 32
+EXP_STEPS = (((0, 2), (2, 4)), ((0, 2), (2, 3), (3, 4)))
 LAST = SLOTS - P
 
 KEYS_AT = 0
@@ -158,15 +159,15 @@ def tile_attend_bias_gate_topk_kernel(tc, qT, k_words, k_scales, vT, vs, kb, og,
         nc.scalar.activation(v_picked[:, :V_SCALAR], listed(v_pool[:], 0, V_SCALAR), ACT.Copy)
 
         neg_max = [sb.tile([P, 1], F32, name="neg_max%d" % b) for b in range(QBLOCKS)]
-        part_total = sb.tile([P, 2, QBLOCKS], F32, name="part_total")
+        part_total = sb.tile([P, 3, QBLOCKS], F32, name="part_total")
         p_rows = []
         for b in range(QBLOCKS):
             nc.vector.tensor_reduce(neg_max[b][:], s_rows[b][:], mybir.AxisListType.X, ALU.max, negate=True)
             p_row = sb.tile([P, PACK, P], F32, name="p_row%d" % b, tag="p_row%d" % b, align_bytes=64)
-            for u in range(2):
+            for u, (t0, t1) in enumerate(EXP_STEPS[b]):
                 nc.scalar.activation(
-                    p_row[:, 2 * u : 2 * u + 2, :],
-                    s_rows[b][:].rearrange("q (s t) -> q t s", t=PACK)[:, 2 * u : 2 * u + 2, :],
+                    p_row[:, t0:t1, :],
+                    s_rows[b][:].rearrange("q (s t) -> q t s", t=PACK)[:, t0:t1, :],
                     ACT.Exp,
                     bias=neg_max[b][:],
                     accum_out=part_total[:, u, b : b + 1],
@@ -207,10 +208,9 @@ def tile_attend_bias_gate_topk_kernel(tc, qT, k_words, k_scales, vT, vs, kb, og,
         nc.scalar.activation(gate[:], half_tanh[:], ACT.Copy, bias=0.5, scale=0.5)
 
         total = sb.tile([P, QBLOCKS], F32, name="total")
-        for b in range(QBLOCKS):
-            nc.scalar.activation(
-                total[:, b : b + 1], part_total[:, 0, b : b + 1], ACT.Identity, bias=part_total[:, 1, b : b + 1]
-            )
+        nc.scalar.activation(total[:, 0:1], part_total[:, 0, 0:1], ACT.Identity, bias=part_total[:, 1, 0:1])
+        nc.scalar.activation(part_total[:, 2, 0:1], part_total[:, 0, 1:2], ACT.Identity, bias=part_total[:, 1, 1:2])
+        nc.scalar.activation(total[:, 1:2], part_total[:, 2, 0:1], ACT.Identity, bias=part_total[:, 2, 1:2])
 
         sums = [ps.tile([P, DV], F32, name="sums%d" % b, tag="sc%d_0" % b) for b in range(QBLOCKS)]
         for b in range(QBLOCKS):

from contextlib import ExitStack

import concourse.mybir as mybir
from concourse.masks import make_identity

F32 = mybir.dt.float32
BF16 = mybir.dt.bfloat16
I32 = mybir.dt.int32
U32 = mybir.dt.uint32
U16 = mybir.dt.uint16
U8 = mybir.dt.uint8
FP8X4 = mybir.dt.float8_e4m3fn_x4
ACT = mybir.ActivationFunctionType
ALU = mybir.AluOpType

P = 128
PACK = 4
QUADRANT = 32
GROUP = 16
LINE = 4
D = 512
SLOTS = 512
POOL = 1024
NQ = 256
DV = 128
CHUNKS = SLOTS // P
QBLOCKS = NQ // P
ROW = P - 1

WIDE_CHUNKS = 0
SCALAR_LINES = 56
V_SCALAR = 160
LEAD = 32
EXP_STEPS = (((0, 2), (2, 4)), ((0, 2), (2, 3), (3, 4)))
LAST = SLOTS - P

KEYS_AT = 0
Q_SCALE_AT = 4 * SLOTS
VALUES_AT = Q_SCALE_AT + NQ
BIAS_ROW_AT = Q_SCALE_AT - 64

FLOPS = 2 * NQ * SLOTS * D + 2 * NQ * SLOTS * DV


def tile_attend_bias_gate_topk_kernel(tc, qT, k_words, k_scales, vT, vs, kb, og, offs, out):
    nc = tc.nc
    with ExitStack() as ctx:
        sb = ctx.enter_context(tc.tile_pool(name="sb", bufs=1))
        shared = ctx.enter_context(tc.tile_pool(name="shared", bufs=1))
        ps = ctx.enter_context(tc.psum_pool(name="ps", bufs=1))

        offsets = sb.tile([P, SLOTS // GROUP], U16, name="offsets")
        nc.sync.dma_start(offsets[:], offs)

        def listed(pool, first, last):
            return pool.indirect(offsets[:, first // GROUP : last // GROUP])

        ks_pool = sb.tile([P, POOL], U8, name="ks_pool", tag="ks_pool", align_bytes=64)
        kb_pool = sb.tile([P, POOL], F32, name="kb_pool", tag="kb_pool", align_bytes=64)
        vs_pool = sb.tile([P, POOL], F32, name="vs_pool")
        ident = sb.tile([P, P], F32, name="ident")
        nc.vector.memset(ks_pool[:].bitcast(I32), 0)
        nc.vector.memset(kb_pool[0:ROW, :], 0.0)
        nc.vector.memset(vs_pool[0:ROW, :], 0.0)
        nc.vector.memset(ident[:], 0.0)
        make_identity(nc, ident[:], nomemset=True)

        nc.scalar.dma_start(kb_pool[ROW:P, :], kb[0:1, :])
        q_raw = sb.tile([P, PACK, NQ], F32, name="q_raw", align_bytes=64)
        nc.sync.dma_start(q_raw[:], qT[0].rearrange("(p t) q -> p t q", t=PACK))
        for a in range(P // QUADRANT):
            nc.sync.dma_start(
                ks_pool[a * QUADRANT : a * QUADRANT + PACK, :].bitcast(I32),
                k_scales[0, a * PACK : (a + 1) * PACK, :].bitcast(I32),
            )
        kw_pool = sb.tile([P, POOL], I32, name="kw_pool", align_bytes=64)
        nc.sync.dma_start(kw_pool[:], k_words[0].rearrange("p n t -> p (n t)").bitcast(I32))
        nc.sync.dma_start(vs_pool[ROW:P, :], vs[0:1, :])
        v_pool = sb.tile([P, POOL], F32, name="v_pool", tag="v_pool")
        nc.sync.dma_start(v_pool[:], vT)

        kb_front = shared.tile([P, LAST], F32, name="kb_front", offset=BIAS_ROW_AT, align_bytes=64)
        vs_row = sb.tile([P, SLOTS], F32, name="vs_row", align_bytes=64)
        kb_last = vs_row[:, LAST:]
        nc.vector.tensor_copy(kb_front[:], listed(kb_pool[:], 0, LAST))
        nc.vector.tensor_copy(kb_last, listed(kb_pool[:], LAST, SLOTS))
        kb_chunks = [kb_front[:, c * P : (c + 1) * P] for c in range(CHUNKS - 1)] + [kb_last]
        kb_turned = ps.tile([P, CHUNKS, P], F32, name="kb_turned", tag="col0")
        for c in range(CHUNKS):
            nc.tensor.transpose(kb_turned[:, CHUNKS - 1 - c, :], kb_chunks[c], ident[:])
        k_scale = sb.tile([P, SLOTS], U8, name="k_scale", align_bytes=64)
        nc.vector.tensor_copy(k_scale[:], listed(ks_pool[:], 0, SLOTS))

        og_sb = sb.tile([P, QBLOCKS, DV], F32, name="og_sb", tag="ks_pool", align_bytes=64)
        nc.sync.dma_start(og_sb[:], og[0].rearrange("(b q) e -> q b e", q=P))

        q_bf = sb.tile([P, NQ * PACK], BF16, name="q_bf", align_bytes=64)
        q_out = q_bf[:].rearrange("p (c i t) -> p c t i", i=LINE, t=PACK)
        q_in = q_raw[:].rearrange("p t (c i) -> p c t i", i=LINE)
        nc.scalar.copy(q_out[:, :SCALAR_LINES], q_in[:, :SCALAR_LINES])
        nc.vector.tensor_copy(q_out[:, SCALAR_LINES:], q_in[:, SCALAR_LINES:])
        q_codes = sb.tile([P, NQ], U32, name="q_codes", align_bytes=64)
        q_scale = shared.tile([P, NQ], U8, name="q_scale", offset=Q_SCALE_AT, align_bytes=64)
        nc.vector.quantize_mx(q_codes[:].bitcast(FP8X4), q_scale[:], q_bf[:])

        nc.scalar.activation(vs_row[:, :LAST], listed(vs_pool[:], 0, LAST), ACT.Copy)

        staging = shared.tile([P, LEAD + SLOTS], BF16, name="staging", offset=VALUES_AT, align_bytes=64)
        v_picked = staging[:, LEAD:]
        kb_cols = staging[:, LEAD - 2 : LEAD - 2 + 2 * CHUNKS].bitcast(F32)
        nc.scalar.copy(kb_cols, kb_turned[:, :, ROW])
        kb_col = [kb_cols[:, CHUNKS - 1 - c : CHUNKS - c] for c in range(CHUNKS)]

        k_picked = shared.tile([P, SLOTS], U32, name="k_picked", offset=KEYS_AT, align_bytes=64)
        in_psum, biased = {}, {}
        for c in range(CHUNKS):
            cols = slice(c * P, (c + 1) * P)
            k_codes = k_picked[:, cols]
            nc.vector.tensor_copy(k_codes, listed(kw_pool[:].bitcast(U32), c * P, (c + 1) * P))
            width = NQ if c < CHUNKS - 1 else P
            for q0 in range(0, NQ, width):
                label = "%d_%d" % (c, q0)
                scores = ps.tile([P, width], F32, name="scores" + label, tag="sc" + label)
                nc.tensor.matmul_mx(
                    scores[:],
                    lhsT=k_codes.bitcast(FP8X4),
                    lhsT_scale=k_scale[:, cols],
                    rhs=q_codes[:, q0 : q0 + width].bitcast(FP8X4),
                    rhs_scale=q_scale[:, q0 : q0 + width],
                    start=True,
                    stop=True,
                )
                if c < WIDE_CHUNKS:
                    wide = sb.tile([P, NQ], F32, name="wide%d" % c, align_bytes=64)
                    nc.scalar.activation(wide[:], scores[:], ACT.Identity, bias=kb_col[c])
                    for b in range(QBLOCKS):
                        biased[c, b] = wide[:, b * P : (b + 1) * P]
                else:
                    for b in range(q0 // P, (q0 + width) // P):
                        in_psum[c, b] = scores[:, b * P - q0 : (b + 1) * P - q0]

        nc.vector.tensor_copy(vs_row[:, LAST:], listed(vs_pool[:], LAST, SLOTS))
        vs_col = sb.tile([P, PACK], F32, name="vs_col", tag="vs_col")
        nc.sync.dma_start(vs_col[:], vs_row[ROW:P, :].rearrange("o (s t) -> o s t", t=PACK))
        nc.vector.tensor_copy(v_picked[:, V_SCALAR:], listed(v_pool[:], V_SCALAR, SLOTS))

        first_block_last_bank = "sc%d_%d" % (CHUNKS - 1, 0)
        second_block_last_bank = "sc%d_%d" % (CHUNKS - 1, P)
        s_rows = []
        for b, tag in enumerate(("row0", first_block_last_bank)):
            s_row = ps.tile([P, SLOTS], F32, name="s_row%d" % b, tag=tag)
            for c in range(CHUNKS):
                if c >= WIDE_CHUNKS:
                    biased[c, b] = sb.tile([P, P], F32, name="biased%d_%d" % (c, b), tag="biased%d_%d" % (c, b), align_bytes=64)[:]
                    nc.scalar.activation(biased[c, b], in_psum[c, b], ACT.Identity, bias=kb_col[c])
                nc.tensor.transpose(s_row[:, c * P : (c + 1) * P], biased[c, b], ident[:])
            s_rows.append(s_row)

        nc.scalar.activation(v_picked[:, :V_SCALAR], listed(v_pool[:], 0, V_SCALAR), ACT.Copy)

        neg_max = [sb.tile([P, 1], F32, name="neg_max%d" % b) for b in range(QBLOCKS)]
        part_total = sb.tile([P, 3, QBLOCKS], F32, name="part_total")
        p_rows = []
        for b in range(QBLOCKS):
            nc.vector.tensor_reduce(neg_max[b][:], s_rows[b][:], mybir.AxisListType.X, ALU.max, negate=True)
            p_row = sb.tile([P, PACK, P], F32, name="p_row%d" % b, tag="p_row%d" % b, align_bytes=64)
            for u, (t0, t1) in enumerate(EXP_STEPS[b]):
                nc.scalar.activation(
                    p_row[:, t0:t1, :],
                    s_rows[b][:].rearrange("q (s t) -> q t s", t=PACK)[:, t0:t1, :],
                    ACT.Exp,
                    bias=neg_max[b][:],
                    accum_out=part_total[:, u, b : b + 1],
                )
            p_rows.append(p_row)

        v_words = v_picked.bitcast(F32)
        v_turned = ps.tile([P, 2, DV], F32, name="v_turned", tag=second_block_last_bank)
        for u in range(2):
            nc.tensor.transpose(v_turned[:, u, :], v_words[:, u : SLOTS // 2 : 2], ident[:])
        v_bf = sb.tile([P, DV * PACK], BF16, name="v_bf", tag="biased3_1", align_bytes=64)
        nc.vector.tensor_copy(
            v_bf[:].bitcast(F32).rearrange("s (e u) -> s e u", u=2), v_turned[:].rearrange("s u e -> s e u")
        )
        v_codes = sb.tile([P, DV], U32, name="v_codes", align_bytes=64)
        v_scale = sb.tile([P, DV], U8, name="v_scale", align_bytes=64)
        nc.vector.quantize_mx(v_codes[:].bitcast(FP8X4), v_scale[:], v_bf[:])

        p_cols = []
        for b in range(QBLOCKS):
            p_col = ps.tile([P, PACK, P], F32, name="p_col%d" % b, tag="col%d" % b)
            for t in range(PACK):
                nc.tensor.transpose(p_col[:, t, :], p_rows[b][:, t, :], ident[:])
            p_cols.append(p_col)

        w_bf = [sb.tile([P, P, PACK], BF16, name="w_bf%d" % b, align_bytes=64) for b in range(QBLOCKS)]
        for b in range(QBLOCKS):
            nc.vector.tensor_tensor(
                w_bf[b][:],
                p_cols[b][:].rearrange("s t q -> s q t"),
                vs_col[:].unsqueeze(1).to_broadcast([P, P, PACK]),
                ALU.mult,
            )

        half_tanh = sb.tile([P, QBLOCKS, DV], F32, name="half_tanh", tag="p_row0", align_bytes=64)
        nc.scalar.activation(half_tanh[:], og_sb[:], ACT.Tanh, scale=0.5)
        gate = sb.tile([P, QBLOCKS, DV], F32, name="gate")
        nc.scalar.activation(gate[:], half_tanh[:], ACT.Copy, bias=0.5, scale=0.5)

        total = sb.tile([P, QBLOCKS], F32, name="total")
        nc.scalar.activation(total[:, 0:1], part_total[:, 0, 0:1], ACT.Identity, bias=part_total[:, 1, 0:1])
        nc.scalar.activation(part_total[:, 2, 0:1], part_total[:, 0, 1:2], ACT.Identity, bias=part_total[:, 1, 1:2])
        nc.scalar.activation(total[:, 1:2], part_total[:, 2, 0:1], ACT.Identity, bias=part_total[:, 2, 1:2])

        sums = [ps.tile([P, DV], F32, name="sums%d" % b, tag="sc%d_0" % b) for b in range(QBLOCKS)]
        for b in range(QBLOCKS):
            w_codes = sb.tile([P, P], U32, name="w_codes%d" % b, tag="p_row1" if b == 0 else "w_codes1", align_bytes=64)
            w_scale = sb.tile([P, P], U8, name="w_scale%d" % b, align_bytes=64)
            nc.vector.quantize_mx(w_codes[:].bitcast(FP8X4), w_scale[:], w_bf[b][:].rearrange("s q t -> s (q t)"))
            nc.tensor.matmul_mx(
                sums[b][:],
                lhsT=w_codes[:].bitcast(FP8X4),
                lhsT_scale=w_scale[:],
                rhs=v_codes[:].bitcast(FP8X4),
                rhs_scale=v_scale[:],
                start=True,
                stop=True,
            )

        inv_total = sb.tile([P, QBLOCKS], F32, name="inv_total", tag="vs_col")
        nc.vector.reciprocal(inv_total[:], total[:])

        for b in range(QBLOCKS):
            result = sb.tile([P, DV], F32, name="result%d" % b)
            nc.vector.scalar_tensor_tensor(
                result[:], sums[b][:], inv_total[:, b : b + 1], gate[:, b, :], ALU.mult, ALU.mult
            )
            nc.sync.dma_start(out[0, b * P : (b + 1) * P, :], result[:])
